import numpy as np, ml_dtypes
CORES = [16,32,48,64,80]
N = 5
import mx_ref
BF = ml_dtypes.bfloat16
def entries(a):
    return np.ascontiguousarray(a.T).reshape(-1)
def table(e):
    return np.ascontiguousarray(np.reshape(e, (-1, 16)).T).astype(np.int32)
def cols(t, e):
    v = np.concatenate([t.reshape(128, -1, 4), np.zeros((128, 1, 4), BF)], axis=1)
    return np.ascontiguousarray(v[:, e]).reshape(128, -1)
def cut(t, i, w=512):
    return t[:, w * i:w * i + w]
def f(rng, *shape):
    return mx_ref.flush((rng.standard_normal(shape, dtype=np.float32) * np.exp2(rng.integers(-2, 3, shape[:-1] + (1,)))).astype(BF))
def wide(rng, *shape, cols=0):
    v = rng.standard_normal(shape, dtype=np.float32) * np.exp2(rng.integers(-12, 13, shape)).astype(np.float32)
    if cols: v *= np.repeat(np.exp2(rng.integers(-cols, cols + 1, shape[:-2] + (1, shape[-1] // 4))) * (rng.random(shape[:-2] + (1, shape[-1] // 4)) > 0.0625), 4, axis=-1).astype(np.float32)
    return mx_ref.flush(v.astype(BF))
TB, T, CAPP, O = 512, 384, 64, 2
def lists(rng, case=""):
    o = []; odd = rng.permutation(N)
    for r in range(N):
        lo, hi = {"one": (1, 1), "full": (CAPP, CAPP), "runs": (1, CAPP // 2), "none": (1, CAPP)}.get(case, (0, CAPP))
        n = rng.integers(lo, hi + 1, N)
        if case == "none":
            if r == odd[0]: n[:] = 0; n[rng.integers(0, N)] = 1
            elif r == odd[1]: n[r] = 0
            elif r == odd[2]: n[np.arange(N) != r] = 0
            else: n[rng.permutation(N)[:rng.integers(1, N)]] = 0
        if n.sum() == 0: n[rng.integers(0, N)] = 1
        if case == "full": named = [np.append([0, TB - 1], 1 + rng.permutation(TB - 2)[:n[q] - 2]) for q in range(N)]
        else: named = [rng.permutation(TB)[:n[q]] for q in range(N)]
        pool = rng.permutation(np.concatenate([q * TB + named[q] for q in range(N)]))
        i = np.arange(len(pool))
        k = T - len(pool)
        i = np.concatenate([i, (rng.random(k) * rng.random(k) * len(pool)).astype(int)])
        i = np.sort(i) if case == "runs" else rng.permutation(i)
        o.append(table(pool[i]))
    return {"want": np.stack(o)}
def setup_inputs(rng):
    return {"x": f(rng, N, 128, 4 * TB), "w": f(rng, N, 128, 512 * O), **lists(rng)}
def setup_inputs_one(rng):
    return {**setup_inputs(rng), **lists(rng, "one")}
def setup_inputs_full(rng):
    return {**setup_inputs(rng), **lists(rng, "full")}
def setup_inputs_runs(rng):
    return {**setup_inputs(rng), **lists(rng, "runs")}
def setup_inputs_none(rng):
    return {**setup_inputs(rng), **lists(rng, "none")}
def setup_inputs_spread(rng):
    d = setup_inputs(rng); d["x"] = wide(rng, N, 128, 4 * TB, cols=8); return d
def check_inputs(d):
    b = []
    for r in range(N):
        e = entries(d["want"][r])
        if e.min() < 0 or e.max() >= N * TB or any(len(np.unique(e[e // TB == q])) > CAPP for q in range(N)): b.append("want")
    return b
def reference(x, w, want):
    every = np.concatenate([x[q] for q in range(N)], axis=1)
    y = np.zeros((N, 128, O * T), np.float32)
    for r in range(N):
        t = mx_ref.quantize(cols(every, entries(want[r])))
        for o in range(O):
            y[r][:, T * o:T * o + T] = mx_ref.matmul(mx_ref.quantize(np.ascontiguousarray(cut(w[r], o))), t)
    return {"y": y}

@@ -1,0 +1,247 @@
+import numpy as np
+from concourse.bass import DstId, RemoteDMATransfer
+from concourse.mybir import dt, AluOpType, AxisListType, ActivationFunctionType
+
+N, TB, NT, CAPP, O = 5, 512, 384, 64, 2
+P = 4
+F32, BF, U16, I32, CODES, PLANE = "float32", "bfloat16", "uint16", "int32", "float8_e4m3fn_x4", "uint8"
+SCRATCH = {}
+for _dt, _bufs in (
+    (F32, "tabp 24 mj 24 scr 24 gm 24 lutk 2560 ii 384 kk 384 nb 3 ab0 128 ab1 256 ab2 384 rr 3 yy 12 "
+          "pf 4 par0 1 t12 1 g1k 1 nq 1 a64 1 i16 24 idx 12 trash 12 mask 32 cr0 8 b1 12 sgn 12 inr 12 tt 12 zero 12 ones 32 "
+          "h0 12 h1 12 ey 12 ev 192 ind 12 nind 12 cc 12 p1 12 rp 32 rt 32 ww 12 mm 32 base 1 zf 32 zt 32 sf 512 cw 512 "
+          "dd 128 dtr 128 lq 4 ls 16 lin 16 fa16 12 fdf 12 sg 384 sgt 384 b1n 24 inrn 24 "
+          "q0 24 q1 24 qa 24 q2 24 qb 24 q3 24 oe 24 oa 24 om 24 oi 24 ov 24 q4 24 oc 24 od 24 py0 640 py1 640 yo 768"),
+    (I32, "tabi 24 pci 1 pbi 4 fi 12 fa 12 fb 12"),
+    (U16, "offk 24 cr 8 hoff 12 zo 12 zu 32 offx 32 fd 24 yoff 24 offo 48"),
+    (BF, "xs 2048 x2 2064 ws 1024 hx 1024 ho 1536"),
+    (CODES, "qw 256 qx 256 qo 384 qr 256"),
+    (PLANE, "sw 256 sx 256 so 384 sr 256"),
+):
+    _w = _bufs.split()
+    for _i in range(0, len(_w), 2):
+        SCRATCH[_w[_i]] = ("sbuf", [128, int(_w[_i + 1])], _dt)
+SCRATCH["pso"] = ("psum", [128, 1024], F32)
+SCRATCH["psr"] = ("psum", [128, 2048], F32)
+SEMAPHORES = ["cv", "cs", "cg", "ct", "dw", "dx", "dwt", "dy", "lloc", "larr", "cloc", "carr0", "carr1"]
+
+
+def rank_program(g, core, T, topo):
+    r = T.rank_of(core)
+    if r is None:
+        return
+    A, AF, X = AluOpType, ActivationFunctionType, AxisListType.X
+    peers = [(r + 1 + a) % N for a in range(P)]
+    eng = {"v": g.vector, "s": g.scalar, "g": g, "t": g.tensor, "y": g.sync}
+    cnt = {"v": 0, "s": 0, "g": 0, "t": 0}
+    seen = {q: {} for q in eng}
+
+    def need(q, deps):
+        for d in deps:
+            if isinstance(d, list):
+                need(q, d)
+                continue
+            sem, val = d
+            if seen[q].get(sem, 0) < val:
+                eng[q].wait_ge(T.sem[sem], val)
+                seen[q][sem] = val
+
+    def op(q, deps, fn, *args, **kw):
+        need(q, deps)
+        cnt[q] += 1
+        fn(*args, **kw).then_inc(T.sem["c" + q], 1)
+        return ("c" + q, cnt[q])
+
+    V, S, G, M = g.vector, g.scalar, g, g.tensor
+
+    for i in range(8):
+        (g.sync if i % 2 == 0 else g.scalar).dma_start(T.tabi[16 * i:16 * i + 16, 0:24], T.want[:, :]).then_inc(T.sem.dw, 16)
+    DW, DX, DWT = ("dw", 128), ("dx", 32), ("dwt", 16)
+    g.sync.dma_start(T.xs[:, :], T.x[:, :]).then_inc(T.sem.dx, 16)
+    g.sync.dma_start(T.x2[:, 14:2062], T.x[:, :]).then_inc(T.sem.dx, 16)
+    g.sync.dma_start(T.ws[:, :], T.w[:, :]).then_inc(T.sem.dwt, 16)
+
+    imp = dict(allow_small_or_imprecise_dtypes=True)
+    PC = op("g", [], G.iota, T.pci[:, :], [[0, 1]], 0, 1)
+    L0 = op("g", [], G.iota, T.lutk[:, 0:256], [[1024, 256]], 0, 0, **imp)
+    II = op("g", [], G.iota, T.ii[:, :], [[1, 384]], 1, 0, **imp)
+    CR0 = op("g", [], G.iota, T.cr0[:, :], [[16, 4], [0, 2]], 0, 0, **imp)
+    I16 = op("g", [], G.iota, T.i16[:, :], [[16, 24]], 0, 0, **imp)
+    PB = [op("v", [PC], V.tensor_scalar, T.pbi[:, 0:1], T.pci[:, :], 15, None, A.bitwise_and),
+          op("v", [], V.tensor_scalar, T.pbi[:, 1:2], T.pci[:, :], 4, 1, A.arith_shift_right, A.bitwise_and),
+          op("v", [], V.tensor_scalar, T.pbi[:, 2:3], T.pci[:, :], 4, None, A.arith_shift_right),
+          op("v", [], V.tensor_scalar, T.pbi[:, 3:4], T.pci[:, :], 31, None, A.bitwise_and)]
+    PF = op("v", [PB], V.tensor_copy, T.pf[:, :], T.pbi[:, :])
+    LO = op("v", [PF], V.tensor_scalar, T.par0[:, :], T.pf[:, 1:2], -1.0, 1.0, A.mult, A.add)
+    T12 = op("v", [PF], V.tensor_scalar, T.t12[:, :], T.pf[:, 3:4], 12.0, float(CAPP), A.mult, A.add)
+    G1K = op("v", [PF], V.tensor_scalar, T.g1k[:, :], T.pf[:, 2:3], 1024.0, None, A.mult)
+    GM = [op("v", [L0, G1K], V.tensor_scalar, T.gm[:, 8 * k:8 * k + 8], T.lutk[:, 0:8], T.g1k[:, 0:1], None, A.is_equal) for k in range(3)]
+    lk = [L0]
+    for k in range(1, 5):
+        lk.append(op("v", [L0], V.tensor_scalar, T.lutk[:, 256 * k:256 * k + 256], T.lutk[:, 0:256], 262144.0 * k, None, A.add))
+    for k in range(5, 10):
+        lk.append(op("s", [L0], S.activation, T.lutk[:, 256 * k:256 * k + 256], T.lutk[:, 0:256], AF.Identity, bias=262144.0 * k))
+
+    OK = op("v", [DW], V.tensor_copy, T.offk[:, :], T.tabi[:, :])
+    MJ = op("v", [GM], V.tensor_tensor, T.mj[:, :], T.tabi[:, :], T.gm[:, :], A.mult)
+    TP = op("v", [], V.tensor_copy, T.tabp[:, :], T.tabi[:, :])
+    KK = op("v", [OK, II, lk], V.tensor_tensor, T.kk[:, :], T.lutk[:, 0:2560].indirect(T.offk[:, 0:24]), T.ii[:, :], A.add)
+    NB = [op("s", [MJ], S.activation, T.scr[:, 8 * k:8 * k + 8], T.mj[:, 8 * k:8 * k + 8], AF.Copy, scale=-1024.0,
+             accum_out=T.nb[:, k:k + 1]) for k in range(3)]
+    EH0 = op("s", [TP, LO], S.activation, T.h0[:, :], T.tabp[:, 0:24:2], AF.Copy, scale=T.par0[:, 0:1])
+    EH1 = op("s", [], S.activation, T.h1[:, :], T.tabp[:, 1:24:2], AF.Copy, scale=T.pf[:, 1:2])
+    IDX = op("s", [II, PF], S.activation, T.idx[:, :], T.ii[:, 0:384:32], AF.Identity, bias=T.pf[:, 3:4])
+    TR = op("s", [T12], S.activation, T.trash[:, :], T.ii[:, 0:12], AF.Identity, bias=T.t12[:, 0:1])
+    NQ = [op("s", [L0], S.activation, T.nq[32 * a:32 * a + 32, :], T.lutk[32 * a:32 * a + 32, 0:1], AF.Identity,
+             bias=-peers[a] - 255.5 / 512, scale=0.0) for a in range(P)]
+    AB2 = op("s", [NB, KK], S.activation, T.ab2[:, :], T.kk[:, 0:384], AF.Abs, bias=T.nb[:, 2:3])
+    AB1 = op("s", [], S.activation, T.ab1[:, :], T.kk[:, 0:256], AF.Abs, bias=T.nb[:, 1:2])
+    AB0 = op("v", [NB, KK], V.tensor_scalar, T.ab0[:, :], T.kk[:, 0:128], T.nb[:, 0:1], None, A.add)
+    EY = op("v", [EH0, EH1], V.tensor_tensor, T.ey[:, :], T.h0[:, :], T.h1[:, :], A.add)
+    MK = op("v", [II, PF], V.tensor_scalar, T.mask[:, :], T.ii[:, 0:32], T.pf[:, 3:4], 0.5, A.subtract, A.is_lt)
+    RR = [op("v", [AB0], V.tensor_reduce, T.rr[:, 0:1], T.ab0[:, :], X, A.min, apply_absolute_value=True)]
+    EHO = op("v", [EY], V.tensor_copy, T.hoff[:, :], T.ey[:, :])
+    RR += [op("v", [AB2], V.tensor_reduce, T.rr[:, 2:3], T.ab2[:, :], X, A.min),
+           op("v", [AB1], V.tensor_reduce, T.rr[:, 1:2], T.ab1[:, :], X, A.min)]
+    B1 = op("s", [EY, NQ], S.activation, T.b1[:, :], T.ey[:, :], AF.Abs, bias=T.nq[:, 0:1], scale=1.0 / 512)
+    SGN = op("s", [B1], S.activation, T.sgn[:, :], T.b1[:, :], AF.Sign, bias=0.5, scale=-1.0)
+    INR = op("s", [SGN], S.activation, T.inr[:, :], T.sgn[:, :], AF.Relu)
+
+    def quarters(place, src, n, deps, give=()):
+        out = []
+        for d in range(P):
+            for a in range(P):
+                o_, i_ = place(d, a), src[32 * a:32 * a + 32, 0:n]
+                if d % 2 == 0 and (d, a) not in give:
+                    out.append(op("v", deps, V.tensor_copy, o_, i_))
+                else:
+                    out.append(op("s", deps, S.activation, o_, i_, AF.Copy))
+        return out
+
+    YY = quarters(lambda d, a: T.yy[32 * d:32 * d + 32, a:12:4], T.rr, 3, [RR])
+    ZZ = op("s", [], S.activation, T.zero[:, :], T.ii[:, 0:12], AF.Copy, scale=0.0)
+    O32 = op("s", [], S.activation, T.ones[:, :], T.ii[:, 0:32], AF.Identity, bias=1.0, scale=0.0)
+    EV = op("s", [EHO, lk], S.activation, T.ev[:, :], T.lutk[:, 0:2560].indirect(T.hoff[:, 0:12]), AF.Copy)
+    CW0 = op("s", [], S.activation, T.cw[:, 0:CAPP], T.ii[:, 0:CAPP], AF.Copy, scale=0.0)
+    TT = op("v", [IDX, INR], V.tensor_tensor, T.tt[:, :], T.idx[:, :], T.inr[:, :], A.mult)
+    IN = op("v", [YY, TT], V.tensor_tensor, T.ind[:, :], T.yy[:, :], T.tt[:, :], A.is_equal)
+    NI = op("v", [], V.tensor_tensor, T.nind[:, :], T.yy[:, :], T.tt[:, :], A.not_equal)
+    CC = op("v", [IN, ZZ], V.tensor_tensor_scan, T.cc[:, :], T.ind[:, :], T.zero[:, :], -1.0, A.add, A.add)
+    P1 = op("v", [NI, TR], V.tensor_tensor, T.p1[:, :], T.nind[:, :], T.trash[:, :], A.mult)
+    RP = op("v", [CC, O32], V.tensor_scalar, T.rp[:, :], T.ones[:, :], T.cc[:, 11:12], None, A.add)
+    WW = op("v", [P1, CC], V.tensor_tensor, T.ww[:, :], T.cc[:, :], T.p1[:, :], A.add)
+    RT = op("v", [RP], V.transpose, T.rt[:, :], T.rp[:, :])
+    MM = op("v", [RT, MK], V.tensor_tensor, T.mm[:, :], T.rt[:, :], T.mask[:, :], A.mult)
+    BS = op("v", [MM], V.tensor_reduce, T.base[:, :], T.mm[:, :], X, A.add)
+    ZO = op("v", [WW, BS], V.tensor_scalar, T.zo[:, :], T.ww[:, :], T.base[:, 0:1], None, A.add)
+    CR = op("v", [CR0, PF], V.tensor_scalar, T.cr[:, :], T.cr0[:, :], T.pf[:, 0:1], None, A.add)
+    CW = op("v", [ZO, EV, CW0], V.tensor_copy, T.cw[:, 0:512].indirect(T.zo[:, 0:12]), T.ev[:, :])
+    DD = op("v", [CW, CR], V.tensor_copy, T.dd[:, :], T.cw[:, 0:CAPP].indirect(T.cr[:, 0:8]))
+    DT = op("v", [DD], V.transpose, T.dtr[:, :], T.dd[:, :])
+    LQ = op("v", [DT], V.tensor_tensor, T.lq[:, :], T.dtr[:, 0:128:32], T.dtr[:, 16:128:32], A.add)
+    LS = quarters(lambda d, a: T.ls[32 * d:32 * d + 32, 4 * a:4 * a + 4], T.lq, 4, [LQ])
+    need("g", [LS])
+
+    def send(items, local):
+        tr = []
+        for j, (a, src, dst, sem) in enumerate(items):
+            c = T.cores[peers[a]]
+            rid, pid, _ = topo.addr(c)
+            es = topo.engines(core, c)
+            n = len(es) // len(items)
+            m = 0
+            for e in es[j * n:j * n + n]:
+                m |= 1 << e
+            tr.append(RemoteDMATransfer(dst_ids=[DstId(rid=rid, pnc=pid)], dma_engine_mask=m, remote_sem=sem, src=src, dst=dst))
+        g.remote_dma_fused(tr, local_sem=local)
+
+    back = [(r - peers[a] - 1) % N for a in range(P)]
+    ne = len(topo.engines(core, T.cores[peers[0]]))
+    send([(a, T.ls[:, 4 * a:4 * a + 4], T.lin[:, 4 * back[a]:4 * back[a] + 4], T.sem.larr) for a in range(P)], T.sem.lloc)
+
+    QW = op("v", [DWT], V.quantize_mx, T.qw[:, :], T.sw[:, :], T.ws[:, :])
+    ZF0 = op("v", [], V.memset, T.zf[:, :], 0.0)
+    FI = op("v", [YY], V.tensor_scalar, T.fi[:, :], T.yy[:, :], -1.0, None, A.add)
+    ZF = [op("v", [ZF0, WW, BS], V.tensor_scalar, T.zf[:, c:c + 12], T.ww[:, :], T.base[:, 0:1], None, A.add) for c in (0, 16)]
+    FA = op("v", [FI], V.tensor_scalar, T.fa[:, :], T.fi[:, :], 31, None, A.bitwise_and)
+    ZT = op("v", [ZF], V.transpose, T.zt[:, :], T.zf[:, :])
+    FB = op("v", [FI], V.tensor_scalar, T.fb[:, :], T.fi[:, :], 5, None, A.arith_shift_right)
+    ZU = op("v", [ZT], V.tensor_copy, T.zu[:, :], T.zt[:, :])
+    SF = op("s", [ZU, lk], S.activation, T.sf[:, :], T.lutk[:, 0:512].indirect(T.zu[:, 0:32]), AF.Copy)
+    OC = op("v", [TP], V.tensor_scalar, T.oc[:, :], T.tabp[:, :], 4.0, float(-4 * TB * r), A.mult, A.add)
+    FA6 = op("v", [FA], V.tensor_scalar, T.fa16[:, :], T.fa[:, :], 16.0, None, A.mult)
+    OD = op("v", [OC], V.tensor_scalar, T.od[:, :], T.oc[:, :], 0.0, float(4 * TB - 4), A.max, A.min)
+    FDF = op("v", [FA6, FB], V.tensor_tensor, T.fdf[:, :], T.fa16[:, :], T.fb[:, :], A.add)
+    OO = [op("v", [OD], V.tensor_scalar, T.offo[:, 24 * t:24 * t + 24], T.od[:, :], float(t), None, A.add) for t in range(2)]
+    FD = [op("v", [FDF], V.tensor_copy, T.fd[:, h:24:2], T.fdf[:, :]) for h in range(2)]
+
+    def gather(t, out, offsets, deps):
+        win = T.xs[:, 0:2046] if t < 2 else T.x2[:, 16:2062]
+        if t < 2:
+            return op("v", [deps[t % 2], DX], V.tensor_copy, out, win.indirect(offsets))
+        return op("s", [deps[t % 2], DX], S.activation, out, win.indirect(offsets), AF.Copy)
+
+    LA = ("larr", ne)
+    OX = [op("v", [LA], V.tensor_scalar, T.offx[:, 16 * t:16 * t + 16], T.lin[:, :], 1.0 / 256, float(t - 4 * TB * r), A.mult, A.add)
+          for t in range(2)]
+    QX = []
+    for h in range(2):
+        HX = [gather(t, T.hx[:, 512 * h + t:512 * h + 512:4], T.offx[:, 16 * (t % 2) + 8 * h:16 * (t % 2) + 8 * h + 8], OX) for t in range(4)]
+        c = slice(128 * h, 128 * h + 128)
+        QX.append(op("v", [HX], V.quantize_mx, T.qx[:, c], T.sx[:, c], T.hx[:, 512 * h:512 * h + 512]))
+        need("g", [QX])
+        pair, sem = (2 * h, 2 * h + 1), T.sem["carr%d" % h]
+        send([(a, T.qx[:, 64 * a:64 * a + 64].bitcast(dt.uint8), T.qr[:, 64 * back[a]:64 * back[a] + 64].bitcast(dt.uint8), sem)
+              for a in pair], T.sem.cloc)
+        send([(a, T.sx[:, 64 * a:64 * a + 64], T.sr[:, 64 * back[a]:64 * back[a] + 64], sem) for a in pair], T.sem.cloc)
+
+    HO_ = [gather(t, T.ho[:, t:1536:4], T.offo[:, 24 * (t % 2):24 * (t % 2) + 24], OO) for t in range(4)]
+    SG = op("s", [FD, SF], S.activation, T.sg[:, :], T.sf[:, 0:512].indirect(T.fd[:, 0:24]), AF.Copy)
+    B1N = op("s", [NQ, TP], S.activation, T.b1n[:, :], T.tabp[:, :], AF.Abs, bias=T.nq[:, 0:1], scale=1.0 / 512)
+    QO = op("v", [HO_], V.quantize_mx, T.qo[:, :], T.so[:, :], T.ho[:, :])
+
+    def product(o, out, codes, plane, deps):
+        return op("t", deps, M.matmul_mx, out, T.qw[:, 128 * o:128 * o + 128], T.sw[:, 128 * o:128 * o + 128], codes, plane, True, True)
+
+    MO = [product(o, T.pso[:, 512 * o:512 * o + 384], T.qo[:, :], T.so[:, :], [QO, QW]) for o in range(O)]
+    A64 = [op("v", [], V.memset, T.a64[32 * a:32 * a + 32, :], float(CAPP * a)) for a in range(P)]
+    OI = op("v", [I16], V.tensor_scalar, T.oi[:, :], T.i16[:, :], T.pf[:, 0:1], float(CAPP * P), A.add, A.add)
+    OE = op("v", [TP], V.tensor_scalar, T.oe[:, :], T.tabp[:, :], float(TB * r), None, A.is_ge)
+    OA = op("v", [TP], V.tensor_scalar, T.oa[:, :], T.tabp[:, :], float(TB * r + TB), None, A.is_lt)
+    SGT = op("v", [SG], V.transpose, T.sgt[:, :], T.sg[:, :])
+    INN = op("v", [B1N], V.tensor_scalar, T.inrn[:, :], T.b1n[:, :], 0.5, None, A.is_lt)
+    Q0 = [op("v", [SGT, A64], V.tensor_scalar, T.q0[:, h:24:2], T.sgt[:, 16 * h:384:32], 1.0 / 1024, T.a64[:, 0:1], A.mult, A.add)
+          for h in range(2)]
+    OM = op("v", [OE, OA], V.tensor_tensor, T.om[:, :], T.oe[:, :], T.oa[:, :], A.mult)
+    Q1 = op("v", [Q0, INN], V.tensor_tensor, T.q1[:, :], T.q0[:, :], T.inrn[:, :], A.mult)
+    QA = [op("v", [Q1], V.tensor_copy, T.qa[64 * h:64 * h + 64, :], T.q1[64 - 64 * h:128 - 64 * h, :]) for h in range(2)]
+    Q2 = op("v", [QA, Q1], V.tensor_tensor, T.q2[:, :], T.q1[:, :], T.qa[:, :], A.add)
+    QB = [op("v", [Q2], V.tensor_copy, T.qb[32 * a:32 * a + 32, :], T.q2[32 * (a ^ 1):32 * (a ^ 1) + 32, :]) for a in range(P)]
+    OV = op("v", [OM, OI], V.tensor_tensor, T.ov[:, :], T.om[:, :], T.oi[:, :], A.mult)
+    Q3 = op("v", [QB, Q2], V.tensor_tensor, T.q3[:, :], T.q2[:, :], T.qb[:, :], A.add)
+    Q4 = op("v", [Q3, OV], V.tensor_tensor, T.q4[:, :], T.q3[:, :], T.ov[:, :], A.add)
+    YO = op("v", [Q4], V.tensor_copy, T.yoff[:, :], T.q4[:, :])
+    PO = [op("v", [MO[0]], V.tensor_copy, T.py0[:, 256:640], T.pso[:, 0:384]),
+          op("s", [MO[1]], S.activation, T.py1[:, 256:640], T.pso[:, 512:896], AF.Copy)]
+
+    PR = [[], []]
+    for h in range(2):
+        c = 64 * min(back[2 * h], back[2 * h + 1])
+        for o in range(O):
+            b = 512 * (2 * h + o)
+            m = product(o, T.psr[:, b:b + 128], T.qr[:, c:c + 128], T.sr[:, c:c + 128], [("carr%d" % h, 2 * ne), QW])
+            if o == 0:
+                PR[0].append(op("v", [m], V.tensor_copy, T.py0[:, c:c + 128], T.psr[:, b:b + 128]))
+            else:
+                PR[1].append(op("s", [m], S.activation, T.py1[:, c:c + 128], T.psr[:, b:b + 128], AF.Copy))
+    nd = 0
+    for h in range(2):
+        c = 192 * h
+        Y0 = op("v", [PR[0], PO[0], YO], V.tensor_copy, T.yo[:, c:c + 192], T.py0[:, 0:640].indirect(T.yoff[:, 12 * h:12 * h + 12]))
+        Y1 = op("s", [PR[1], PO[1], YO], S.activation, T.yo[:, 384 + c:384 + c + 192], T.py1[:, 0:640].indirect(T.yoff[:, 12 * h:12 * h + 12]), AF.Copy)
+        for o, tok in ((0, Y0), (1, Y1)):
+            need("y", [tok])
+            g.sync.dma_start(T.y[:, 384 * o + c:384 * o + c + 192], T.yo[:, 384 * o + c:384 * o + c + 192]).then_inc(T.sem.dy, 16)
+            nd += 16
+    need("y", [("dy", nd)])
+    need("g", [("lloc", ne), ("cloc", 4 * ne)] + [("c" + q, cnt[q]) for q in cnt])

@@ -4,19 +4,18 @@ from concourse.mybir import dt, AluOpType, AxisListType, ActivationFunctionType
 
 N, TB, NT, CAPP, O = 5, 512, 384, 64, 2
 P = 4
+NV = N * TB
+L0 = 128
 F32, BF, U16, I32, CODES, PLANE = "float32", "bfloat16", "uint16", "int32", "float8_e4m3fn_x4", "uint8"
 SCRATCH = {}
 for _dt, _bufs in (
-    (F32, "tabp 24 mj 24 scr 24 gm 24 lutk 2560 ii 384 kk 384 nb 3 ab0 128 ab1 256 ab2 384 rr 3 yy 12 "
-          "pf 4 par0 1 t12 1 g1k 1 nq 1 a64 1 i16 24 idx 12 trash 12 mask 32 cr0 8 b1 12 sgn 12 inr 12 tt 12 zero 12 ones 32 "
-          "h0 12 h1 12 ey 12 ev 192 ind 12 nind 12 cc 12 p1 12 rp 32 rt 32 ww 12 mm 32 base 1 zf 32 zt 32 sf 512 cw 512 "
-          "dd 128 dtr 128 lq 4 ls 16 lin 16 fa16 12 fdf 12 sg 384 sgt 384 b1n 24 inrn 24 "
-          "q0 24 q1 24 qa 24 q2 24 qb 24 q3 24 oe 24 oa 24 om 24 oi 24 ov 24 q4 24 oc 24 od 24 py0 640 py1 640 yo 768"),
-    (I32, "tabi 24 pci 1 pbi 4 fi 12 fa 12 fb 12"),
-    (U16, "offk 24 cr 8 hoff 12 zo 12 zu 32 offx 32 fd 24 yoff 24 offo 48"),
-    (BF, "xs 2048 x2 2064 ws 1024 hx 1024 ho 1536"),
-    (CODES, "qw 256 qx 256 qo 384 qr 256"),
-    (PLANE, "sw 256 sx 256 so 384 sr 256"),
+    (F32, "tb 2944 ct 160 wrap 1 mask 32 peer 1 cr0 8 trash 12 ney 16 inr 12 ind 12 big 12 cc 12 p1 12 ww 12 rp 32 rt 32 base 1 "
+          "ev 192 cw 1696 dd 128 dtr 128 lq 4 sval 256 sg 384 sgt 384 py0 768 py1 768 yo 768"),
+    (I32, "tabi 40 sh 16"),
+    (U16, "offk 24 coff 2 c2 2 cr 8 hoff 16 zo 12 ls 16 lin 16 gl 16 fd 32 yoff 24"),
+    (BF, "ones 256 step 384 da 384 sc 1440 xs 2048 xt 2048 ws 1024 hx 1024"),
+    (CODES, "qw 256 qx 256 qo 512 qr 256"),
+    (PLANE, "sw 256 sx 256 so 512 sr 256"),
 ):
     _w = _bufs.split()
     for _i in range(0, len(_w), 2):
@@ -54,92 +53,85 @@ def rank_program(g, core, T, topo):
 
     V, S, G, M = g.vector, g.scalar, g, g.tensor
 
+    def lut(a, b, s=1):
+        return T.tb[:, L0 + a:L0 + b:s]
+
+    def quarter(a):
+        return slice(32 * a, 32 * a + 32)
+
     for i in range(8):
         (g.sync if i % 2 == 0 else g.scalar).dma_start(T.tabi[16 * i:16 * i + 16, 0:24], T.want[:, :]).then_inc(T.sem.dw, 16)
-    DW, DX, DWT = ("dw", 128), ("dx", 32), ("dwt", 16)
+    DW, DX, DWT = ("dw", 128), ("dx", 16), ("dwt", 16)
     g.sync.dma_start(T.xs[:, :], T.x[:, :]).then_inc(T.sem.dx, 16)
-    g.sync.dma_start(T.x2[:, 14:2062], T.x[:, :]).then_inc(T.sem.dx, 16)
     g.sync.dma_start(T.ws[:, :], T.w[:, :]).then_inc(T.sem.dwt, 16)
 
     imp = dict(allow_small_or_imprecise_dtypes=True)
-    PC = op("g", [], G.iota, T.pci[:, :], [[0, 1]], 0, 1)
-    L0 = op("g", [], G.iota, T.lutk[:, 0:256], [[1024, 256]], 0, 0, **imp)
-    II = op("g", [], G.iota, T.ii[:, :], [[1, 384]], 1, 0, **imp)
+    blocks = ([[16, 2], [128, 4], [32, 4]], 1), ([[16, 2], [0, 4], [32, 4]], 1), ([[0, 2], [1, 16]], 0), ([[1, 2], [2, 8], [0, 2]], 0)
+    BL = [op("g", [], G.iota, T.tb[:, 32 * b:32 * b + 32], pat, 0, cm, **imp) for b, (pat, cm) in enumerate(blocks)]
+    PAD = op("g", [], G.iota, T.tabi[:, 24:40], [[0, 16]], 0, 0)
+    ON = op("v", [], V.memset, T.ones[:, :], 1.0)
+    ZS = op("v", [], V.memset, T.step[:, 128:384], 0.0)
+    SEED = op("v", [ON], V.tensor_tensor_scan, lut(0, 256), T.ones[:, :], T.ones[:, :], -1.0, A.mult, A.add)
+    ID = op("g", [ON], G.affine_select, T.step[:, 0:128], T.ones[:, 0:128], [[-1, 128]], A.is_equal, 0.0, 0, 1)
+    PEER = [ID]
+    for a in range(P):
+        PEER.append(op("g", [PEER[-1]], G.iota, T.peer[quarter(a), :], [[0, 1]], peers[a], 0, **imp))
+    TR = op("g", [PEER], G.iota, T.trash[:, :], [[1, 12]], CAPP + 1, 12, **imp)
     CR0 = op("g", [], G.iota, T.cr0[:, :], [[16, 4], [0, 2]], 0, 0, **imp)
-    I16 = op("g", [], G.iota, T.i16[:, :], [[16, 24]], 0, 0, **imp)
-    PB = [op("v", [PC], V.tensor_scalar, T.pbi[:, 0:1], T.pci[:, :], 15, None, A.bitwise_and),
-          op("v", [], V.tensor_scalar, T.pbi[:, 1:2], T.pci[:, :], 4, 1, A.arith_shift_right, A.bitwise_and),
-          op("v", [], V.tensor_scalar, T.pbi[:, 2:3], T.pci[:, :], 4, None, A.arith_shift_right),
-          op("v", [], V.tensor_scalar, T.pbi[:, 3:4], T.pci[:, :], 31, None, A.bitwise_and)]
-    PF = op("v", [PB], V.tensor_copy, T.pf[:, :], T.pbi[:, :])
-    LO = op("v", [PF], V.tensor_scalar, T.par0[:, :], T.pf[:, 1:2], -1.0, 1.0, A.mult, A.add)
-    T12 = op("v", [PF], V.tensor_scalar, T.t12[:, :], T.pf[:, 3:4], 12.0, float(CAPP), A.mult, A.add)
-    G1K = op("v", [PF], V.tensor_scalar, T.g1k[:, :], T.pf[:, 2:3], 1024.0, None, A.mult)
-    GM = [op("v", [L0, G1K], V.tensor_scalar, T.gm[:, 8 * k:8 * k + 8], T.lutk[:, 0:8], T.g1k[:, 0:1], None, A.is_equal) for k in range(3)]
-    lk = [L0]
-    for k in range(1, 5):
-        lk.append(op("v", [L0], V.tensor_scalar, T.lutk[:, 256 * k:256 * k + 256], T.lutk[:, 0:256], 262144.0 * k, None, A.add))
+    CW0 = op("g", [], G.iota, T.cw[:, 0:CAPP], [[1, CAPP]], NV, 2, **imp)
+    SV = op("g", [], G.iota, T.sval[:, :], [[1, P * CAPP]], TB * r + TB, 0, **imp)
+    lk = [SEED]
     for k in range(5, 10):
-        lk.append(op("s", [L0], S.activation, T.lutk[:, 256 * k:256 * k + 256], T.lutk[:, 0:256], AF.Identity, bias=262144.0 * k))
+        lk.append(op("s", [SEED], S.activation, lut(256 * k, 256 * k + 256), lut(0, 256), AF.Identity, bias=256.0 * k))
+    for k in range(1, 4):
+        lk.append(op("v", [SEED], V.tensor_scalar, lut(256 * k, 256 * k + 256), lut(0, 256), 256.0 * k, None, A.add))
+    CT = op("v", [BL, SEED], V.transpose, T.ct[:, :], T.tb[:, 0:160])
+    lk.append(op("v", [], V.tensor_scalar, lut(1024, 1280), lut(0, 256), 1024.0, None, A.add))
+    WR = op("v", [CT], V.tensor_scalar, T.wrap[:, :], T.ct[:, 32:33], 128.0, -8.0, A.is_ge, A.mult)
+    MK = op("v", [CT], V.tensor_scalar, T.mask[:, :], lut(0, 32), T.ct[:, 128:129], None, A.is_gt)
+    CO = op("v", [WR], V.tensor_scalar, T.coff[:, 0:1], T.ct[:, 0:1], 1.0 / 16, T.wrap[:, 0:1], A.mult, A.add)
 
-    OK = op("v", [DW], V.tensor_copy, T.offk[:, :], T.tabi[:, :])
-    MJ = op("v", [GM], V.tensor_tensor, T.mj[:, :], T.tabi[:, :], T.gm[:, :], A.mult)
-    TP = op("v", [], V.tensor_copy, T.tabp[:, :], T.tabi[:, :])
-    KK = op("v", [OK, II, lk], V.tensor_tensor, T.kk[:, :], T.lutk[:, 0:2560].indirect(T.offk[:, 0:24]), T.ii[:, :], A.add)
-    NB = [op("s", [MJ], S.activation, T.scr[:, 8 * k:8 * k + 8], T.mj[:, 8 * k:8 * k + 8], AF.Copy, scale=-1024.0,
-             accum_out=T.nb[:, k:k + 1]) for k in range(3)]
-    EH0 = op("s", [TP, LO], S.activation, T.h0[:, :], T.tabp[:, 0:24:2], AF.Copy, scale=T.par0[:, 0:1])
-    EH1 = op("s", [], S.activation, T.h1[:, :], T.tabp[:, 1:24:2], AF.Copy, scale=T.pf[:, 1:2])
-    IDX = op("s", [II, PF], S.activation, T.idx[:, :], T.ii[:, 0:384:32], AF.Identity, bias=T.pf[:, 3:4])
-    TR = op("s", [T12], S.activation, T.trash[:, :], T.ii[:, 0:12], AF.Identity, bias=T.t12[:, 0:1])
-    NQ = [op("s", [L0], S.activation, T.nq[32 * a:32 * a + 32, :], T.lutk[32 * a:32 * a + 32, 0:1], AF.Identity,
-             bias=-peers[a] - 255.5 / 512, scale=0.0) for a in range(P)]
-    AB2 = op("s", [NB, KK], S.activation, T.ab2[:, :], T.kk[:, 0:384], AF.Abs, bias=T.nb[:, 2:3])
-    AB1 = op("s", [], S.activation, T.ab1[:, :], T.kk[:, 0:256], AF.Abs, bias=T.nb[:, 1:2])
-    AB0 = op("v", [NB, KK], V.tensor_scalar, T.ab0[:, :], T.kk[:, 0:128], T.nb[:, 0:1], None, A.add)
-    EY = op("v", [EH0, EH1], V.tensor_tensor, T.ey[:, :], T.h0[:, :], T.h1[:, :], A.add)
-    MK = op("v", [II, PF], V.tensor_scalar, T.mask[:, :], T.ii[:, 0:32], T.pf[:, 3:4], 0.5, A.subtract, A.is_lt)
-    RR = [op("v", [AB0], V.tensor_reduce, T.rr[:, 0:1], T.ab0[:, :], X, A.min, apply_absolute_value=True)]
-    EHO = op("v", [EY], V.tensor_copy, T.hoff[:, :], T.ey[:, :])
-    RR += [op("v", [AB2], V.tensor_reduce, T.rr[:, 2:3], T.ab2[:, :], X, A.min),
-           op("v", [AB1], V.tensor_reduce, T.rr[:, 1:2], T.ab1[:, :], X, A.min)]
-    B1 = op("s", [EY, NQ], S.activation, T.b1[:, :], T.ey[:, :], AF.Abs, bias=T.nq[:, 0:1], scale=1.0 / 512)
-    SGN = op("s", [B1], S.activation, T.sgn[:, :], T.b1[:, :], AF.Sign, bias=0.5, scale=-1.0)
-    INR = op("s", [SGN], S.activation, T.inr[:, :], T.sgn[:, :], AF.Relu)
-
-    def quarters(place, src, n, deps, give=()):
-        out = []
-        for d in range(P):
-            for a in range(P):
-                o_, i_ = place(d, a), src[32 * a:32 * a + 32, 0:n]
-                if d % 2 == 0 and (d, a) not in give:
-                    out.append(op("v", deps, V.tensor_copy, o_, i_))
-                else:
-                    out.append(op("s", deps, S.activation, o_, i_, AF.Copy))
-        return out
-
-    YY = quarters(lambda d, a: T.yy[32 * d:32 * d + 32, a:12:4], T.rr, 3, [RR])
-    ZZ = op("s", [], S.activation, T.zero[:, :], T.ii[:, 0:12], AF.Copy, scale=0.0)
-    O32 = op("s", [], S.activation, T.ones[:, :], T.ii[:, 0:32], AF.Identity, bias=1.0, scale=0.0)
-    EV = op("s", [EHO, lk], S.activation, T.ev[:, :], T.lutk[:, 0:2560].indirect(T.hoff[:, 0:12]), AF.Copy)
-    CW0 = op("s", [], S.activation, T.cw[:, 0:CAPP], T.ii[:, 0:CAPP], AF.Copy, scale=0.0)
-    TT = op("v", [IDX, INR], V.tensor_tensor, T.tt[:, :], T.idx[:, :], T.inr[:, :], A.mult)
-    IN = op("v", [YY, TT], V.tensor_tensor, T.ind[:, :], T.yy[:, :], T.tt[:, :], A.is_equal)
-    NI = op("v", [], V.tensor_tensor, T.nind[:, :], T.yy[:, :], T.tt[:, :], A.not_equal)
-    CC = op("v", [IN, ZZ], V.tensor_tensor_scan, T.cc[:, :], T.ind[:, :], T.zero[:, :], -1.0, A.add, A.add)
-    P1 = op("v", [NI, TR], V.tensor_tensor, T.p1[:, :], T.nind[:, :], T.trash[:, :], A.mult)
-    RP = op("v", [CC, O32], V.tensor_scalar, T.rp[:, :], T.ones[:, :], T.cc[:, 11:12], None, A.add)
-    WW = op("v", [P1, CC], V.tensor_tensor, T.ww[:, :], T.cc[:, :], T.p1[:, :], A.add)
+    tab = T.tabi[:, 0:40]
+    EY = op("v", [DW, CO, PAD], V.tensor_scalar, T.ney[:, :], tab.indirect(T.coff[:, 0:1]), -1.0, None, A.mult)
+    OK = op("v", [], V.tensor_copy, T.offk[:, :], T.tabi[:, 0:24])
+    win = lut(0, NV)
+    DA = op("s", [OK, EY, lk], S.activation, T.da[:, :], win.indirect(T.offk[:, 0:24]), AF.Abs, bias=T.ney[:, 0:1])
+    DC = op("s", [], S.activation, T.sc[:, 384:512], win.indirect(T.offk[:, 16:24]), AF.Abs, bias=T.ney[:, 8:9])
+    DB = op("v", [OK, EY, lk], V.tensor_scalar, T.sc[:, 768:1024], win.indirect(T.offk[:, 8:24]), T.ney[:, 4:5], 0.0, A.add, A.not_equal)
+    SH = op("v", [], V.tensor_scalar, T.sh[:, :], tab.indirect(T.coff[:, 0:1]), 9, None, A.arith_shift_right)
+    SB = op("v", [DB, ZS, ID], V.tensor_tensor_scan, T.sc[:, 512:768], T.sc[:, 768:1024], T.step[:, 0:256], 0.0, A.min, A.add)
+    INR = op("v", [SH, PEER], V.tensor_scalar, T.inr[:, :], T.sh[:, 0:12], T.peer[:, 0:1], None, A.is_equal)
+    SA = op("v", [DA], V.tensor_tensor_scan, T.sc[:, 0:384], T.da[:, :], T.step[:, :], 0.0, A.min, A.add)
+    SC = op("v", [DC], V.tensor_tensor_scan, T.sc[:, 1024:1152], T.sc[:, 384:512], T.step[:, 0:128], 0.0, A.min, A.add)
+    X1 = [op("v", [SA, SB, SC], V.tensor_copy, T.sc[0:64, 575:1440:384], T.sc[64:128, 383:1152:384]),
+          op("s", [SA, SB, SC], S.activation, T.sc[64:128, 575:1440:384], T.sc[0:64, 383:1152:384], AF.Copy)]
+    X2 = []
+    for d in range(P):
+        o_, i_ = T.sc[quarter(d), 479:1440:192], T.sc[quarter((d + 1) % P), 383:1344:192]
+        X2.append(op("v", [X1], V.tensor_copy, o_, i_) if d % 2 else op("s", [X1], S.activation, o_, i_, AF.Copy))
+    HO = op("v", [], V.tensor_copy, T.hoff[:, :], tab.indirect(T.coff[:, 0:1]))
+    IN = op("v", [X2, INR], V.tensor_tensor, T.ind[:, :], T.sc[:, 383:1440:96], T.inr[:, :], A.mult)
+    BG = op("s", [IN], S.activation, T.big[:, :], T.ind[:, :], AF.Identity, bias=4096.0, scale=-4096.0)
+    EV = op("s", [HO], S.activation, T.ev[:, :], win.indirect(T.hoff[:, 0:12]), AF.Copy)
+    CC = op("v", [IN], V.tensor_tensor_scan, T.cc[:, :], T.ind[:, :], T.step[:, 128:140], 0.0, A.add, A.add)
+    CR = op("v", [CR0], V.tensor_scalar, T.cr[:, :], T.cr0[:, :], T.ct[:, 64:65], None, A.add)
+    RP = op("v", [CC, MK], V.tensor_scalar, T.rp[:, :], T.mask[:, :], T.cc[:, 11:12], None, A.mult)
+    P1 = op("v", [BG, TR], V.tensor_tensor, T.p1[:, :], T.big[:, :], T.trash[:, :], A.min)
     RT = op("v", [RP], V.transpose, T.rt[:, :], T.rp[:, :])
-    MM = op("v", [RT, MK], V.tensor_tensor, T.mm[:, :], T.rt[:, :], T.mask[:, :], A.mult)
-    BS = op("v", [MM], V.tensor_reduce, T.base[:, :], T.mm[:, :], X, A.add)
-    ZO = op("v", [WW, BS], V.tensor_scalar, T.zo[:, :], T.ww[:, :], T.base[:, 0:1], None, A.add)
-    CR = op("v", [CR0, PF], V.tensor_scalar, T.cr[:, :], T.cr0[:, :], T.pf[:, 0:1], None, A.add)
-    CW = op("v", [ZO, EV, CW0], V.tensor_copy, T.cw[:, 0:512].indirect(T.zo[:, 0:12]), T.ev[:, :])
+    WW = op("v", [P1], V.tensor_tensor, T.ww[:, :], T.cc[:, :], T.p1[:, :], A.add)
+    BS = op("v", [RT], V.tensor_reduce, T.base[:, :], T.rt[:, :], X, A.add)
+    ZO = op("v", [WW, BS], V.tensor_scalar, T.zo[:, :], T.ww[:, :], T.base[:, 0:1], -1.0, A.add, A.add)
+    CW = op("v", [ZO, EV, CW0], V.tensor_copy, T.cw[:, :].indirect(T.zo[:, 0:12]), T.ev[:, :])
     DD = op("v", [CW, CR], V.tensor_copy, T.dd[:, :], T.cw[:, 0:CAPP].indirect(T.cr[:, 0:8]))
     DT = op("v", [DD], V.transpose, T.dtr[:, :], T.dd[:, :])
-    LQ = op("v", [DT], V.tensor_tensor, T.lq[:, :], T.dtr[:, 0:128:32], T.dtr[:, 16:128:32], A.add)
-    LS = quarters(lambda d, a: T.ls[32 * d:32 * d + 32, 4 * a:4 * a + 4], T.lq, 4, [LQ])
+    LQ = op("v", [DT], V.tensor_tensor, T.lq[:, :], T.dtr[:, 0:128:32], T.dtr[:, 16:128:32], A.min)
+
+    def spread(buf, first):
+        one = op("v", [first], V.tensor_copy, buf[32:64, :], buf[0:32, :])
+        return op("v", [one], V.tensor_copy, buf[64:128, :], buf[0:64, :])
+
+    LS = spread(T.ls, [op("v", [LQ], V.tensor_scalar, T.ls[0:32, 4 * a:4 * a + 4], T.lq[quarter(a), :], float(-TB * peers[a]),
+                          float(TB - 1), A.add, A.min) for a in range(P)])
     need("g", [LS])
 
     def send(items, local):
@@ -159,34 +151,25 @@ def rank_program(g, core, T, topo):
     ne = len(topo.engines(core, T.cores[peers[0]]))
     send([(a, T.ls[:, 4 * a:4 * a + 4], T.lin[:, 4 * back[a]:4 * back[a] + 4], T.sem.larr) for a in range(P)], T.sem.lloc)
 
+    XT = [op("s", [DX], S.activation, T.xt[:, TB * t:TB * t + TB], T.xs[:, t:4 * TB:4], AF.Copy) for t in range(4)]
+    QO = op("v", [DX], V.quantize_mx, T.qo[:, :], T.so[:, :], T.xs[:, :])
+    C2 = op("v", [], V.tensor_scalar, T.c2[:, :], lut(0, 32, 16), T.ct[:, 96:97], 23.0, A.add, A.min)
+    GL = spread(T.gl, [op("v", [], V.tensor_copy, T.gl[0:32, 4 * a:4 * a + 4], T.lq[quarter(a), :]) for a in range(P)])
+    FD = op("v", [C2], V.tensor_copy, T.fd[:, :], tab.indirect(T.c2[:, 0:2]))
     QW = op("v", [DWT], V.quantize_mx, T.qw[:, :], T.sw[:, :], T.ws[:, :])
-    ZF0 = op("v", [], V.memset, T.zf[:, :], 0.0)
-    FI = op("v", [YY], V.tensor_scalar, T.fi[:, :], T.yy[:, :], -1.0, None, A.add)
-    ZF = [op("v", [ZF0, WW, BS], V.tensor_scalar, T.zf[:, c:c + 12], T.ww[:, :], T.base[:, 0:1], None, A.add) for c in (0, 16)]
-    FA = op("v", [FI], V.tensor_scalar, T.fa[:, :], T.fi[:, :], 31, None, A.bitwise_and)
-    ZT = op("v", [ZF], V.transpose, T.zt[:, :], T.zf[:, :])
-    FB = op("v", [FI], V.tensor_scalar, T.fb[:, :], T.fi[:, :], 5, None, A.arith_shift_right)
-    ZU = op("v", [ZT], V.tensor_copy, T.zu[:, :], T.zt[:, :])
-    SF = op("s", [ZU, lk], S.activation, T.sf[:, :], T.lutk[:, 0:512].indirect(T.zu[:, 0:32]), AF.Copy)
-    OC = op("v", [TP], V.tensor_scalar, T.oc[:, :], T.tabp[:, :], 4.0, float(-4 * TB * r), A.mult, A.add)
-    FA6 = op("v", [FA], V.tensor_scalar, T.fa16[:, :], T.fa[:, :], 16.0, None, A.mult)
-    OD = op("v", [OC], V.tensor_scalar, T.od[:, :], T.oc[:, :], 0.0, float(4 * TB - 4), A.max, A.min)
-    FDF = op("v", [FA6, FB], V.tensor_tensor, T.fdf[:, :], T.fa16[:, :], T.fb[:, :], A.add)
-    OO = [op("v", [OD], V.tensor_scalar, T.offo[:, 24 * t:24 * t + 24], T.od[:, :], float(t), None, A.add) for t in range(2)]
-    FD = [op("v", [FDF], V.tensor_copy, T.fd[:, h:24:2], T.fdf[:, :]) for h in range(2)]
 
-    def gather(t, out, offsets, deps):
-        win = T.xs[:, 0:2046] if t < 2 else T.x2[:, 16:2062]
-        if t < 2:
-            return op("v", [deps[t % 2], DX], V.tensor_copy, out, win.indirect(offsets))
-        return op("s", [deps[t % 2], DX], S.activation, out, win.indirect(offsets), AF.Copy)
+    def product(o, out, codes, plane, deps):
+        return op("t", deps, M.matmul_mx, out, T.qw[:, 128 * o:128 * o + 128], T.sw[:, 128 * o:128 * o + 128], codes, plane, True, True)
+
+    MO = [product(o, T.pso[:, 512 * o:512 * o + 512], T.qo[:, :], T.so[:, :], [QO, QW]) for o in range(O)]
 
     LA = ("larr", ne)
-    OX = [op("v", [LA], V.tensor_scalar, T.offx[:, 16 * t:16 * t + 16], T.lin[:, :], 1.0 / 256, float(t - 4 * TB * r), A.mult, A.add)
-          for t in range(2)]
     QX = []
     for h in range(2):
-        HX = [gather(t, T.hx[:, 512 * h + t:512 * h + 512:4], T.offx[:, 16 * (t % 2) + 8 * h:16 * (t % 2) + 8 * h + 8], OX) for t in range(4)]
+        HX = []
+        for t in range(4):
+            o_, i_ = T.hx[:, 512 * h + t:512 * h + 512:4], T.xt[:, TB * t:TB * t + TB].indirect(T.lin[:, 8 * h:8 * h + 8])
+            HX.append(op("v", [LA, XT[t]], V.tensor_copy, o_, i_) if t < 2 else op("s", [LA, XT[t]], S.activation, o_, i_, AF.Copy))
         c = slice(128 * h, 128 * h + 128)
         QX.append(op("v", [HX], V.quantize_mx, T.qx[:, c], T.sx[:, c], T.hx[:, 512 * h:512 * h + 512]))
         need("g", [QX])
@@ -195,34 +178,11 @@ def rank_program(g, core, T, topo):
               for a in pair], T.sem.cloc)
         send([(a, T.sx[:, 64 * a:64 * a + 64], T.sr[:, 64 * back[a]:64 * back[a] + 64], sem) for a in pair], T.sem.cloc)
 
-    HO_ = [gather(t, T.ho[:, t:1536:4], T.offo[:, 24 * (t % 2):24 * (t % 2) + 24], OO) for t in range(4)]
-    SG = op("s", [FD, SF], S.activation, T.sg[:, :], T.sf[:, 0:512].indirect(T.fd[:, 0:24]), AF.Copy)
-    B1N = op("s", [NQ, TP], S.activation, T.b1n[:, :], T.tabp[:, :], AF.Abs, bias=T.nq[:, 0:1], scale=1.0 / 512)
-    QO = op("v", [HO_], V.quantize_mx, T.qo[:, :], T.so[:, :], T.ho[:, :])
-
-    def product(o, out, codes, plane, deps):
-        return op("t", deps, M.matmul_mx, out, T.qw[:, 128 * o:128 * o + 128], T.sw[:, 128 * o:128 * o + 128], codes, plane, True, True)
-
-    MO = [product(o, T.pso[:, 512 * o:512 * o + 384], T.qo[:, :], T.so[:, :], [QO, QW]) for o in range(O)]
-    A64 = [op("v", [], V.memset, T.a64[32 * a:32 * a + 32, :], float(CAPP * a)) for a in range(P)]
-    OI = op("v", [I16], V.tensor_scalar, T.oi[:, :], T.i16[:, :], T.pf[:, 0:1], float(CAPP * P), A.add, A.add)
-    OE = op("v", [TP], V.tensor_scalar, T.oe[:, :], T.tabp[:, :], float(TB * r), None, A.is_ge)
-    OA = op("v", [TP], V.tensor_scalar, T.oa[:, :], T.tabp[:, :], float(TB * r + TB), None, A.is_lt)
+    PO = [op("s", [MO[o]], S.activation, T["py%d" % o][:, 0:TB], T.pso[:, 512 * o:512 * o + 512], AF.Copy) for o in range(O)]
+    GS = op("v", [GL, SV, EV, DA, DC], V.tensor_copy, lut(0, NV + P * CAPP).indirect(T.gl[:, 0:16]), T.sval[:, :])
+    SG = op("s", [GS, FD], S.activation, T.sg[:, :], win.indirect(T.fd[:, 0:24]), AF.Copy)
     SGT = op("v", [SG], V.transpose, T.sgt[:, :], T.sg[:, :])
-    INN = op("v", [B1N], V.tensor_scalar, T.inrn[:, :], T.b1n[:, :], 0.5, None, A.is_lt)
-    Q0 = [op("v", [SGT, A64], V.tensor_scalar, T.q0[:, h:24:2], T.sgt[:, 16 * h:384:32], 1.0 / 1024, T.a64[:, 0:1], A.mult, A.add)
-          for h in range(2)]
-    OM = op("v", [OE, OA], V.tensor_tensor, T.om[:, :], T.oe[:, :], T.oa[:, :], A.mult)
-    Q1 = op("v", [Q0, INN], V.tensor_tensor, T.q1[:, :], T.q0[:, :], T.inrn[:, :], A.mult)
-    QA = [op("v", [Q1], V.tensor_copy, T.qa[64 * h:64 * h + 64, :], T.q1[64 - 64 * h:128 - 64 * h, :]) for h in range(2)]
-    Q2 = op("v", [QA, Q1], V.tensor_tensor, T.q2[:, :], T.q1[:, :], T.qa[:, :], A.add)
-    QB = [op("v", [Q2], V.tensor_copy, T.qb[32 * a:32 * a + 32, :], T.q2[32 * (a ^ 1):32 * (a ^ 1) + 32, :]) for a in range(P)]
-    OV = op("v", [OM, OI], V.tensor_tensor, T.ov[:, :], T.om[:, :], T.oi[:, :], A.mult)
-    Q3 = op("v", [QB, Q2], V.tensor_tensor, T.q3[:, :], T.q2[:, :], T.qb[:, :], A.add)
-    Q4 = op("v", [Q3, OV], V.tensor_tensor, T.q4[:, :], T.q3[:, :], T.ov[:, :], A.add)
-    YO = op("v", [Q4], V.tensor_copy, T.yoff[:, :], T.q4[:, :])
-    PO = [op("v", [MO[0]], V.tensor_copy, T.py0[:, 256:640], T.pso[:, 0:384]),
-          op("s", [MO[1]], S.activation, T.py1[:, 256:640], T.pso[:, 512:896], AF.Copy)]
+    YO = op("v", [SGT], V.tensor_scalar, T.yoff[:, :], T.sgt[:, 0:384:16], float(-TB * r), None, A.add)
 
     PR = [[], []]
     for h in range(2):
@@ -231,14 +191,14 @@ def rank_program(g, core, T, topo):
             b = 512 * (2 * h + o)
             m = product(o, T.psr[:, b:b + 128], T.qr[:, c:c + 128], T.sr[:, c:c + 128], [("carr%d" % h, 2 * ne), QW])
             if o == 0:
-                PR[0].append(op("v", [m], V.tensor_copy, T.py0[:, c:c + 128], T.psr[:, b:b + 128]))
+                PR[0].append(op("v", [m], V.tensor_copy, T.py0[:, TB + c:TB + c + 128], T.psr[:, b:b + 128]))
             else:
-                PR[1].append(op("s", [m], S.activation, T.py1[:, c:c + 128], T.psr[:, b:b + 128], AF.Copy))
+                PR[1].append(op("s", [m], S.activation, T.py1[:, TB + c:TB + c + 128], T.psr[:, b:b + 128], AF.Copy))
     nd = 0
     for h in range(2):
         c = 192 * h
-        Y0 = op("v", [PR[0], PO[0], YO], V.tensor_copy, T.yo[:, c:c + 192], T.py0[:, 0:640].indirect(T.yoff[:, 12 * h:12 * h + 12]))
-        Y1 = op("s", [PR[1], PO[1], YO], S.activation, T.yo[:, 384 + c:384 + c + 192], T.py1[:, 0:640].indirect(T.yoff[:, 12 * h:12 * h + 12]), AF.Copy)
+        Y0 = op("v", [PR[0], PO[0], YO], V.tensor_copy, T.yo[:, c:c + 192], T.py0[:, :].indirect(T.yoff[:, 12 * h:12 * h + 12]))
+        Y1 = op("s", [PR[1], PO[1], YO], S.activation, T.yo[:, 384 + c:384 + c + 192], T.py1[:, :].indirect(T.yoff[:, 12 * h:12 * h + 12]), AF.Copy)
         for o, tok in ((0, Y0), (1, Y1)):
             need("y", [tok])
             g.sync.dma_start(T.y[:, 384 * o + c:384 * o + c + 192], T.yo[:, 384 * o + c:384 * o + c + 192]).then_inc(T.sem.dy, 16)

@@ -6,23 +6,25 @@ N, TB, NT, CAPP, O = 5, 512, 384, 64, 2
 P = 4
 NV = N * TB
 L0 = 128
+STEPS = ((0,), (1, 2), (3,))
+MARK = 0.75
 F32, BF, U16, I32, CODES, PLANE = "float32", "bfloat16", "uint16", "int32", "float8_e4m3fn_x4", "uint8"
 SCRATCH = {}
 for _dt, _bufs in (
-    (F32, "tb 2944 ct 160 wrap 1 mask 32 peer 1 cr0 8 trash 12 ney 16 inr 12 ind 12 big 12 cc 12 p1 12 ww 12 rp 32 rt 32 base 1 "
-          "ev 192 cw 1696 dd 128 dtr 128 lq 4 sval 256 sg 384 sgt 384 py0 768 py1 768 yo 768"),
-    (I32, "tabi 40 sh 16"),
+    (F32, "tb 2944 ct 160 wrap 1 mask 32 peer 1 cr0 8 trash 12 ney 16 ind 12 big 12 cc 12 p1 12 ww 12 rp 32 rt 32 base 1 "
+          "ev 192 cw 1696 dd 128 dtr 128 lq 4 glf 16 sval 256 sg 384 sgt 384 py0 768 py1 768 yo 768"),
+    (I32, "tabi 40"),
     (U16, "offk 24 coff 2 c2 2 cr 8 hoff 16 zo 12 ls 16 lin 16 gl 16 fd 32 yoff 24"),
-    (BF, "ones 256 step 384 da 384 sc 1440 xs 2048 xt 2048 ws 1024 hx 1024"),
-    (CODES, "qw 256 qx 256 qo 512 qr 256"),
-    (PLANE, "sw 256 sx 256 so 512 sr 256"),
+    (BF, "ones 128 step 384 th 12 da 384 sc 1440 xs 2048 xt 3072 ws 1024"),
+    (CODES, "qw 256 qx 512 qo 512 qr 256"),
+    (PLANE, "sw 256 sx 512 so 512 sr 256"),
 ):
     _w = _bufs.split()
     for _i in range(0, len(_w), 2):
         SCRATCH[_w[_i]] = ("sbuf", [128, int(_w[_i + 1])], _dt)
 SCRATCH["pso"] = ("psum", [128, 1024], F32)
 SCRATCH["psr"] = ("psum", [128, 2048], F32)
-SEMAPHORES = ["cv", "cs", "cg", "ct", "dw", "dx", "dwt", "dy", "lloc", "larr", "cloc", "carr0", "carr1"]
+SEMAPHORES = ["cv", "cs", "cg", "ct", "dw", "dx", "dwt", "dy", "lloc", "larr0", "larr1", "larr2", "cloc", "carr0", "carr1"]
 
 
 def rank_program(g, core, T, topo):
@@ -31,6 +33,8 @@ def rank_program(g, core, T, topo):
         return
     A, AF, X = AluOpType, ActivationFunctionType, AxisListType.X
     peers = [(r + 1 + a) % N for a in range(P)]
+    back = [(r - peers[a] - 1) % N for a in range(P)]
+    ne = len(topo.engines(core, T.cores[peers[0]]))
     eng = {"v": g.vector, "s": g.scalar, "g": g, "t": g.tensor, "y": g.sync}
     cnt = {"v": 0, "s": 0, "g": 0, "t": 0}
     seen = {q: {} for q in eng}
@@ -51,6 +55,19 @@ def rank_program(g, core, T, topo):
         fn(*args, **kw).then_inc(T.sem["c" + q], 1)
         return ("c" + q, cnt[q])
 
+    def send(items, local, part=0, parts=1):
+        tr = []
+        for j, (a, src, dst, sem) in enumerate(items):
+            c = T.cores[peers[a]]
+            rid, pid, _ = topo.addr(c)
+            es = topo.engines(core, c)[ne * part // parts:ne * (part + 1) // parts]
+            n = len(es) // len(items)
+            m = 0
+            for e in es[j * n:j * n + n]:
+                m |= 1 << e
+            tr.append(RemoteDMATransfer(dst_ids=[DstId(rid=rid, pnc=pid)], dma_engine_mask=m, remote_sem=sem, src=src, dst=dst))
+        g.remote_dma_fused(tr, local_sem=local)
+
     V, S, G, M = g.vector, g.scalar, g, g.tensor
 
     def lut(a, b, s=1):
@@ -60,7 +77,7 @@ def rank_program(g, core, T, topo):
         return slice(32 * a, 32 * a + 32)
 
     for i in range(8):
-        (g.sync if i % 2 == 0 else g.scalar).dma_start(T.tabi[16 * i:16 * i + 16, 0:24], T.want[:, :]).then_inc(T.sem.dw, 16)
+        (g.scalar if i % 4 == 1 else g.sync).dma_start(T.tabi[16 * i:16 * i + 16, 0:24], T.want[:, :]).then_inc(T.sem.dw, 16)
     DW, DX, DWT = ("dw", 128), ("dx", 16), ("dwt", 16)
     g.sync.dma_start(T.xs[:, :], T.x[:, :]).then_inc(T.sem.dx, 16)
     g.sync.dma_start(T.ws[:, :], T.w[:, :]).then_inc(T.sem.dwt, 16)
@@ -68,40 +85,45 @@ def rank_program(g, core, T, topo):
     imp = dict(allow_small_or_imprecise_dtypes=True)
     blocks = ([[16, 2], [128, 4], [32, 4]], 1), ([[16, 2], [0, 4], [32, 4]], 1), ([[0, 2], [1, 16]], 0), ([[1, 2], [2, 8], [0, 2]], 0)
     BL = [op("g", [], G.iota, T.tb[:, 32 * b:32 * b + 32], pat, 0, cm, **imp) for b, (pat, cm) in enumerate(blocks)]
-    PAD = op("g", [], G.iota, T.tabi[:, 24:40], [[0, 16]], 0, 0)
     ON = op("v", [], V.memset, T.ones[:, :], 1.0)
+    SEED = op("v", [ON], V.tensor_tensor_scan, lut(0, 128), T.ones[:, :], T.ones[:, :], -1.0, A.mult, A.add)
+    S2 = op("v", [SEED], V.tensor_scalar, lut(128, 256), lut(0, 128), 128.0, None, A.add)
     ZS = op("v", [], V.memset, T.step[:, 128:384], 0.0)
-    SEED = op("v", [ON], V.tensor_tensor_scan, lut(0, 256), T.ones[:, :], T.ones[:, :], -1.0, A.mult, A.add)
-    ID = op("g", [ON], G.affine_select, T.step[:, 0:128], T.ones[:, 0:128], [[-1, 128]], A.is_equal, 0.0, 0, 1)
+    PAD = op("g", [], G.iota, T.tabi[:, 24:40], [[0, 16]], 0, 0)
+    CR0 = op("g", [], G.iota, T.cr0[:, :], [[16, 4], [0, 2]], 0, 0, **imp)
+    ID = op("g", [ZS], G.affine_select, T.step[:, 0:128], T.step[:, 128:256], [[-1, 128]], A.not_equal, MARK, 0, 1)
     PEER = [ID]
     for a in range(P):
-        PEER.append(op("g", [PEER[-1]], G.iota, T.peer[quarter(a), :], [[0, 1]], peers[a], 0, **imp))
+        PEER.append(op("g", [PEER[-1]], G.iota, T.peer[quarter(a), :], [[0, 1]], 2 * TB * peers[a] + TB - 1 - int(MARK * 2 ** 18), 0, **imp))
     TR = op("g", [PEER], G.iota, T.trash[:, :], [[1, 12]], CAPP + 1, 12, **imp)
-    CR0 = op("g", [], G.iota, T.cr0[:, :], [[16, 4], [0, 2]], 0, 0, **imp)
     CW0 = op("g", [], G.iota, T.cw[:, 0:CAPP], [[1, CAPP]], NV, 2, **imp)
     SV = op("g", [], G.iota, T.sval[:, :], [[1, P * CAPP]], TB * r + TB, 0, **imp)
-    lk = [SEED]
-    for k in range(5, 10):
-        lk.append(op("s", [SEED], S.activation, lut(256 * k, 256 * k + 256), lut(0, 256), AF.Identity, bias=256.0 * k))
-    for k in range(1, 4):
-        lk.append(op("v", [SEED], V.tensor_scalar, lut(256 * k, 256 * k + 256), lut(0, 256), 256.0 * k, None, A.add))
-    CT = op("v", [BL, SEED], V.transpose, T.ct[:, :], T.tb[:, 0:160])
-    lk.append(op("v", [], V.tensor_scalar, lut(1024, 1280), lut(0, 256), 1024.0, None, A.add))
+
+    def grow(q, deps, a, n):
+        if q == "v":
+            return op(q, deps, V.tensor_scalar, lut(a, a + n), lut(0, n), float(a), None, A.add)
+        return op(q, deps, S.activation, lut(a, a + n), lut(0, n), AF.Identity, bias=float(a))
+
+    lk = [grow("s", [SEED], a, 128) for a in (1024, 1152)] + [grow("s", [S2], 256 * k, 256) for k in range(5, 10)]
+    lk += [grow("v", [S2], 256 * k, 256) for k in range(1, 3)]
+    CT = op("v", [BL], V.transpose, T.ct[:, :], T.tb[:, 0:160])
+    lk.append(grow("v", [], 768, 256))
     WR = op("v", [CT], V.tensor_scalar, T.wrap[:, :], T.ct[:, 32:33], 128.0, -8.0, A.is_ge, A.mult)
-    MK = op("v", [CT], V.tensor_scalar, T.mask[:, :], lut(0, 32), T.ct[:, 128:129], None, A.is_gt)
+    MK = op("v", [], V.tensor_scalar, T.mask[:, :], lut(0, 32), T.ct[:, 128:129], None, A.is_gt)
     CO = op("v", [WR], V.tensor_scalar, T.coff[:, 0:1], T.ct[:, 0:1], 1.0 / 16, T.wrap[:, 0:1], A.mult, A.add)
+    CR = op("v", [CR0], V.tensor_scalar, T.cr[:, :], T.cr0[:, :], T.ct[:, 64:65], None, A.add)
 
     tab = T.tabi[:, 0:40]
-    EY = op("v", [DW, CO, PAD], V.tensor_scalar, T.ney[:, :], tab.indirect(T.coff[:, 0:1]), -1.0, None, A.mult)
-    OK = op("v", [], V.tensor_copy, T.offk[:, :], T.tabi[:, 0:24])
+    OK = op("v", [DW], V.tensor_copy, T.offk[:, :], T.tabi[:, 0:24])
+    EY = op("v", [CO, PAD], V.tensor_scalar, T.ney[:, :], tab.indirect(T.coff[:, 0:1]), -2.0, None, A.mult)
     win = lut(0, NV)
-    DA = op("s", [OK, EY, lk], S.activation, T.da[:, :], win.indirect(T.offk[:, 0:24]), AF.Abs, bias=T.ney[:, 0:1])
-    DC = op("s", [], S.activation, T.sc[:, 384:512], win.indirect(T.offk[:, 16:24]), AF.Abs, bias=T.ney[:, 8:9])
-    DB = op("v", [OK, EY, lk], V.tensor_scalar, T.sc[:, 768:1024], win.indirect(T.offk[:, 8:24]), T.ney[:, 4:5], 0.0, A.add, A.not_equal)
-    SH = op("v", [], V.tensor_scalar, T.sh[:, :], tab.indirect(T.coff[:, 0:1]), 9, None, A.arith_shift_right)
-    SB = op("v", [DB, ZS, ID], V.tensor_tensor_scan, T.sc[:, 512:768], T.sc[:, 768:1024], T.step[:, 0:256], 0.0, A.min, A.add)
-    INR = op("v", [SH, PEER], V.tensor_scalar, T.inr[:, :], T.sh[:, 0:12], T.peer[:, 0:1], None, A.is_equal)
+    DA = op("s", [OK, EY, lk], S.activation, T.da[:, :], win.indirect(T.offk[:, 0:24]), AF.Abs, bias=T.ney[:, 0:1], scale=2.0)
+    DC = op("s", [], S.activation, T.sc[:, 384:512], win.indirect(T.offk[:, 16:24]), AF.Abs, bias=T.ney[:, 8:9], scale=2.0)
+    DB = op("v", [OK, EY, lk], V.tensor_scalar, T.sc[:, 768:1024], win.indirect(T.offk[:, 8:24]), -2.0, T.ney[:, 4:5], A.mult, A.not_equal)
+    HO = op("v", [], V.tensor_copy, T.hoff[:, :], tab.indirect(T.coff[:, 0:1]))
+    SB = op("v", [DB, ID], V.tensor_tensor_scan, T.sc[:, 512:768], T.sc[:, 768:1024], T.step[:, 0:256], 0.0, A.min, A.add)
     SA = op("v", [DA], V.tensor_tensor_scan, T.sc[:, 0:384], T.da[:, :], T.step[:, :], 0.0, A.min, A.add)
+    TH = op("v", [PEER], V.tensor_scalar, T.th[:, :], T.ney[:, 0:12], T.peer[:, 0:1], -2.0 ** -18, A.add, A.mult)
     SC = op("v", [DC], V.tensor_tensor_scan, T.sc[:, 1024:1152], T.sc[:, 384:512], T.step[:, 0:128], 0.0, A.min, A.add)
     X1 = [op("v", [SA, SB, SC], V.tensor_copy, T.sc[0:64, 575:1440:384], T.sc[64:128, 383:1152:384]),
           op("s", [SA, SB, SC], S.activation, T.sc[64:128, 575:1440:384], T.sc[0:64, 383:1152:384], AF.Copy)]
@@ -109,12 +131,10 @@ def rank_program(g, core, T, topo):
     for d in range(P):
         o_, i_ = T.sc[quarter(d), 479:1440:192], T.sc[quarter((d + 1) % P), 383:1344:192]
         X2.append(op("v", [X1], V.tensor_copy, o_, i_) if d % 2 else op("s", [X1], S.activation, o_, i_, AF.Copy))
-    HO = op("v", [], V.tensor_copy, T.hoff[:, :], tab.indirect(T.coff[:, 0:1]))
-    IN = op("v", [X2, INR], V.tensor_tensor, T.ind[:, :], T.sc[:, 383:1440:96], T.inr[:, :], A.mult)
+    IN = op("v", [X2, TH], V.tensor_tensor, T.ind[:, :], T.sc[:, 383:1440:96], T.th[:, :], A.is_equal)
     BG = op("s", [IN], S.activation, T.big[:, :], T.ind[:, :], AF.Identity, bias=4096.0, scale=-4096.0)
     EV = op("s", [HO], S.activation, T.ev[:, :], win.indirect(T.hoff[:, 0:12]), AF.Copy)
     CC = op("v", [IN], V.tensor_tensor_scan, T.cc[:, :], T.ind[:, :], T.step[:, 128:140], 0.0, A.add, A.add)
-    CR = op("v", [CR0], V.tensor_scalar, T.cr[:, :], T.cr0[:, :], T.ct[:, 64:65], None, A.add)
     RP = op("v", [CC, MK], V.tensor_scalar, T.rp[:, :], T.mask[:, :], T.cc[:, 11:12], None, A.mult)
     P1 = op("v", [BG, TR], V.tensor_tensor, T.p1[:, :], T.big[:, :], T.trash[:, :], A.min)
     RT = op("v", [RP], V.transpose, T.rt[:, :], T.rp[:, :])
@@ -126,36 +146,26 @@ def rank_program(g, core, T, topo):
     DT = op("v", [DD], V.transpose, T.dtr[:, :], T.dd[:, :])
     LQ = op("v", [DT], V.tensor_tensor, T.lq[:, :], T.dtr[:, 0:128:32], T.dtr[:, 16:128:32], A.min)
 
-    def spread(buf, first):
-        one = op("v", [first], V.tensor_copy, buf[32:64, :], buf[0:32, :])
-        return op("v", [one], V.tensor_copy, buf[64:128, :], buf[0:64, :])
+    def local(a, d):
+        return op("v", [LQ], V.tensor_scalar, T.ls[quarter(d), 4 * a:4 * a + 4], T.lq[quarter(a), :], float(-TB * peers[a]),
+                  float(TB - 1), A.add, A.min)
 
-    LS = spread(T.ls, [op("v", [LQ], V.tensor_scalar, T.ls[0:32, 4 * a:4 * a + 4], T.lq[quarter(a), :], float(-TB * peers[a]),
-                          float(TB - 1), A.add, A.min) for a in range(P)])
-    need("g", [LS])
-
-    def send(items, local):
-        tr = []
-        for j, (a, src, dst, sem) in enumerate(items):
-            c = T.cores[peers[a]]
-            rid, pid, _ = topo.addr(c)
-            es = topo.engines(core, c)
-            n = len(es) // len(items)
-            m = 0
-            for e in es[j * n:j * n + n]:
-                m |= 1 << e
-            tr.append(RemoteDMATransfer(dst_ids=[DstId(rid=rid, pnc=pid)], dma_engine_mask=m, remote_sem=sem, src=src, dst=dst))
-        g.remote_dma_fused(tr, local_sem=local)
-
-    back = [(r - peers[a] - 1) % N for a in range(P)]
-    ne = len(topo.engines(core, T.cores[peers[0]]))
-    send([(a, T.ls[:, 4 * a:4 * a + 4], T.lin[:, 4 * back[a]:4 * back[a] + 4], T.sem.larr) for a in range(P)], T.sem.lloc)
+    LS = [local(P - 1, d) for d in range(P)]
+    L1 = [local(a, 0) for a in range(P - 1)]
+    for k, step in enumerate(STEPS):
+        need("g", [LS])
+        send([(back[b], T.ls[:, 4 * back[b]:4 * back[b] + 4], T.lin[:, 4 * b:4 * b + 4], T.sem["larr%d" % k]) for b in step], T.sem.lloc)
+        if k == 0:
+            LS = [op("v", [L1], V.tensor_copy, T.ls[quarter(d), 0:12], T.ls[0:32, 0:12]) for d in range(1, P)]
 
     XT = [op("s", [DX], S.activation, T.xt[:, TB * t:TB * t + TB], T.xs[:, t:4 * TB:4], AF.Copy) for t in range(4)]
-    QO = op("v", [DX], V.quantize_mx, T.qo[:, :], T.so[:, :], T.xs[:, :])
+    G0 = [op("s", [LQ], S.activation, T.glf[0:32, 4 * a:4 * a + 4], T.lq[quarter(a), :], AF.Copy) for a in range(P)]
+    G1 = [op("s", [G0], S.activation, T.glf[quarter(d), :], T.glf[0:32, :], AF.Copy) for d in range(1, P)]
     C2 = op("v", [], V.tensor_scalar, T.c2[:, :], lut(0, 32, 16), T.ct[:, 96:97], 23.0, A.add, A.min)
-    GL = spread(T.gl, [op("v", [], V.tensor_copy, T.gl[0:32, 4 * a:4 * a + 4], T.lq[quarter(a), :]) for a in range(P)])
+    QO = op("v", [DX], V.quantize_mx, T.qo[:, :], T.so[:, :], T.xs[:, :])
+    GL = op("v", [G1], V.tensor_copy, T.gl[:, :], T.glf[:, :])
     FD = op("v", [C2], V.tensor_copy, T.fd[:, :], tab.indirect(T.c2[:, 0:2]))
+    GS = op("v", [GL, SV, EV], V.tensor_copy, lut(0, NV + P * CAPP).indirect(T.gl[:, 0:16]), T.sval[:, :])
     QW = op("v", [DWT], V.quantize_mx, T.qw[:, :], T.sw[:, :], T.ws[:, :])
 
     def product(o, out, codes, plane, deps):
@@ -163,45 +173,42 @@ def rank_program(g, core, T, topo):
 
     MO = [product(o, T.pso[:, 512 * o:512 * o + 512], T.qo[:, :], T.so[:, :], [QO, QW]) for o in range(O)]
 
-    LA = ("larr", ne)
-    QX = []
-    for h in range(2):
-        HX = []
+    for k, step in enumerate(STEPS):
+        lo, hi = step[0], step[-1] + 1
+        HX, LA, e = [], ("larr%d" % k, ne), 4 * TB + 256 * hi
         for t in range(4):
-            o_, i_ = T.hx[:, 512 * h + t:512 * h + 512:4], T.xt[:, TB * t:TB * t + TB].indirect(T.lin[:, 8 * h:8 * h + 8])
+            o_, i_ = T.xt[:, 4 * TB + 256 * lo + t:e:4], T.xt[:, TB * t:TB * t + TB].indirect(T.lin[:, 4 * lo:4 * hi])
             HX.append(op("v", [LA, XT[t]], V.tensor_copy, o_, i_) if t < 2 else op("s", [LA, XT[t]], S.activation, o_, i_, AF.Copy))
-        c = slice(128 * h, 128 * h + 128)
-        QX.append(op("v", [HX], V.quantize_mx, T.qx[:, c], T.sx[:, c], T.hx[:, 512 * h:512 * h + 512]))
-        need("g", [QX])
-        pair, sem = (2 * h, 2 * h + 1), T.sem["carr%d" % h]
-        send([(a, T.qx[:, 64 * a:64 * a + 64].bitcast(dt.uint8), T.qr[:, 64 * back[a]:64 * back[a] + 64].bitcast(dt.uint8), sem)
-              for a in pair], T.sem.cloc)
-        send([(a, T.sx[:, 64 * a:64 * a + 64], T.sr[:, 64 * back[a]:64 * back[a] + 64], sem) for a in pair], T.sem.cloc)
+        need("g", [op("v", [HX], V.quantize_mx, T.qx[:, 128 * k:128 * k + 128], T.sx[:, 128 * k:128 * k + 128], T.xt[:, e - 512:e])])
+        col = {a: slice(128 * k + 128 - 64 * (hi - a), 128 * k + 192 - 64 * (hi - a)) for a in step}
+        sem = T.sem["carr%d" % (k == len(STEPS) - 1)]
+        send([(a, T.qx[:, col[a]].bitcast(dt.uint8), T.qr[:, 64 * back[a]:64 * back[a] + 64].bitcast(dt.uint8), sem) for a in step], T.sem.cloc)
+        send([(a, T.sx[:, col[a]], T.sr[:, 64 * back[a]:64 * back[a] + 64], sem) for a in step], T.sem.cloc)
 
-    PO = [op("s", [MO[o]], S.activation, T["py%d" % o][:, 0:TB], T.pso[:, 512 * o:512 * o + 512], AF.Copy) for o in range(O)]
-    GS = op("v", [GL, SV, EV, DA, DC], V.tensor_copy, lut(0, NV + P * CAPP).indirect(T.gl[:, 0:16]), T.sval[:, :])
     SG = op("s", [GS, FD], S.activation, T.sg[:, :], win.indirect(T.fd[:, 0:24]), AF.Copy)
+    PO = [None, op("s", [MO[1]], S.activation, T.py1[:, 0:TB], T.pso[:, 512:1024], AF.Copy)]
+    PO[0] = op("v", [MO[0]], V.tensor_copy, T.py0[:, 0:TB], T.pso[:, 0:512])
     SGT = op("v", [SG], V.transpose, T.sgt[:, :], T.sg[:, :])
     YO = op("v", [SGT], V.tensor_scalar, T.yoff[:, :], T.sgt[:, 0:384:16], float(-TB * r), None, A.add)
 
     PR = [[], []]
-    for h in range(2):
-        c = 64 * min(back[2 * h], back[2 * h + 1])
-        for o in range(O):
+    for h, (c, n, new, calls) in enumerate(((64, 192, 192, 2 * len(STEPS) - 2), (0, 128, 64, 2))):
+        for o in (1, 0):
             b = 512 * (2 * h + o)
-            m = product(o, T.psr[:, b:b + 128], T.qr[:, c:c + 128], T.sr[:, c:c + 128], [("carr%d" % h, 2 * ne), QW])
+            m = product(o, T.psr[:, b:b + n], T.qr[:, c:c + n], T.sr[:, c:c + n], [("carr%d" % h, calls * ne), QW])
             if o == 0:
-                PR[0].append(op("v", [m], V.tensor_copy, T.py0[:, TB + c:TB + c + 128], T.psr[:, b:b + 128]))
+                PR[0].append(op("v", [m], V.tensor_copy, T.py0[:, TB + c:TB + c + new], T.psr[:, b:b + new]))
             else:
-                PR[1].append(op("s", [m], S.activation, T.py1[:, TB + c:TB + c + 128], T.psr[:, b:b + 128], AF.Copy))
+                PR[1].append(op("s", [m], S.activation, T.py1[:, TB + c:TB + c + new], T.psr[:, b:b + new], AF.Copy))
     nd = 0
-    for h in range(2):
-        c = 192 * h
-        Y0 = op("v", [PR[0], PO[0], YO], V.tensor_copy, T.yo[:, c:c + 192], T.py0[:, :].indirect(T.yoff[:, 12 * h:12 * h + 12]))
-        Y1 = op("s", [PR[1], PO[1], YO], S.activation, T.yo[:, 384 + c:384 + c + 192], T.py1[:, :].indirect(T.yoff[:, 12 * h:12 * h + 12]), AF.Copy)
-        for o, tok in ((0, Y0), (1, Y1)):
-            need("y", [tok])
-            g.sync.dma_start(T.y[:, 384 * o + c:384 * o + c + 192], T.yo[:, 384 * o + c:384 * o + c + 192]).then_inc(T.sem.dy, 16)
+    for h, (a, b) in enumerate(((0, 14), (14, 24))):
+        c, e = 16 * a, 16 * b
+        Y1 = op("s", [PR[1], PO[1], YO], S.activation, T.yo[:, NT + c:NT + e], T.py1[:, :].indirect(T.yoff[:, a:b]), AF.Copy)
+        Y0 = op("v", [PR[0], PO[0], YO], V.tensor_copy, T.yo[:, c:e], T.py0[:, :].indirect(T.yoff[:, a:b]))
+        for o, tok in ((1, Y1), (0, Y0)):
+            q = "s" if h and o else "y"
+            need(q, [tok])
+            eng[q].dma_start(T.y[:, NT * o + c:NT * o + e], T.yo[:, NT * o + c:NT * o + e]).then_inc(T.sem.dy, 16)
             nd += 16
     need("y", [("dy", nd)])
-    need("g", [("lloc", ne), ("cloc", 4 * ne)] + [("c" + q, cnt[q]) for q in cnt])
+    need("g", [("lloc", len(STEPS) * ne), ("cloc", 2 * len(STEPS) * ne)] + [("c" + q, cnt[q]) for q in cnt])

import numpy as np
from concourse.bass import DstId, RemoteDMATransfer
from concourse.mybir import dt, AluOpType, AxisListType, ActivationFunctionType

N, TB, NT, CAPP, O = 5, 512, 384, 64, 2
P = 4
NV = N * TB
L0 = 128
STEPS = ((0,), (1, 2), (3,))
MARK = 0.75
F32, BF, U16, I32, CODES, PLANE = "float32", "bfloat16", "uint16", "int32", "float8_e4m3fn_x4", "uint8"
SCRATCH = {}
for _dt, _bufs in (
    (F32, "tb 2944 ct 160 wrap 1 mask 32 peer 1 cr0 8 trash 12 ney 16 ind 12 big 12 cc 12 p1 12 ww 12 rp 32 rt 32 base 1 "
          "ev 192 cw 1696 dd 128 dtr 128 lq 4 glf 16 sval 256 sg 384 sgt 384 py0 768 py1 768 yo 768"),
    (I32, "tabi 40"),
    (U16, "offk 24 coff 2 c2 2 cr 8 hoff 16 zo 12 ls 16 lin 16 gl 16 fd 32 yoff 24"),
    (BF, "ones 128 step 384 th 12 da 384 sc 1440 xs 2048 xt 3072 ws 1024"),
    (CODES, "qw 256 qx 512 qo 512 qr 256"),
    (PLANE, "sw 256 sx 512 so 512 sr 256"),
):
    _w = _bufs.split()
    for _i in range(0, len(_w), 2):
        SCRATCH[_w[_i]] = ("sbuf", [128, int(_w[_i + 1])], _dt)
SCRATCH["pso"] = ("psum", [128, 1024], F32)
SCRATCH["psr"] = ("psum", [128, 2048], F32)
SEMAPHORES = ["cv", "cs", "cg", "ct", "dw", "dx", "dwt", "dy", "lloc", "larr0", "larr1", "larr2", "cloc", "carr0", "carr1"]


def rank_program(g, core, T, topo):
    r = T.rank_of(core)
    if r is None:
        return
    A, AF, X = AluOpType, ActivationFunctionType, AxisListType.X
    peers = [(r + 1 + a) % N for a in range(P)]
    back = [(r - peers[a] - 1) % N for a in range(P)]
    ne = len(topo.engines(core, T.cores[peers[0]]))
    eng = {"v": g.vector, "s": g.scalar, "g": g, "t": g.tensor, "y": g.sync}
    cnt = {"v": 0, "s": 0, "g": 0, "t": 0}
    seen = {q: {} for q in eng}

    def need(q, deps):
        for d in deps:
            if isinstance(d, list):
                need(q, d)
                continue
            sem, val = d
            if seen[q].get(sem, 0) < val:
                eng[q].wait_ge(T.sem[sem], val)
                seen[q][sem] = val

    def op(q, deps, fn, *args, **kw):
        need(q, deps)
        cnt[q] += 1
        fn(*args, **kw).then_inc(T.sem["c" + q], 1)
        return ("c" + q, cnt[q])

    def send(items, local, part=0, parts=1):
        tr = []
        for j, (a, src, dst, sem) in enumerate(items):
            c = T.cores[peers[a]]
            rid, pid, _ = topo.addr(c)
            es = topo.engines(core, c)[ne * part // parts:ne * (part + 1) // parts]
            n = len(es) // len(items)
            m = 0
            for e in es[j * n:j * n + n]:
                m |= 1 << e
            tr.append(RemoteDMATransfer(dst_ids=[DstId(rid=rid, pnc=pid)], dma_engine_mask=m, remote_sem=sem, src=src, dst=dst))
        g.remote_dma_fused(tr, local_sem=local)

    V, S, G, M = g.vector, g.scalar, g, g.tensor

    def lut(a, b, s=1):
        return T.tb[:, L0 + a:L0 + b:s]

    def quarter(a):
        return slice(32 * a, 32 * a + 32)

    for i in range(8):
        (g.scalar if i % 4 == 1 else g.sync).dma_start(T.tabi[16 * i:16 * i + 16, 0:24], T.want[:, :]).then_inc(T.sem.dw, 16)
    DW, DX, DWT = ("dw", 128), ("dx", 16), ("dwt", 16)
    g.sync.dma_start(T.xs[:, :], T.x[:, :]).then_inc(T.sem.dx, 16)
    g.sync.dma_start(T.ws[:, :], T.w[:, :]).then_inc(T.sem.dwt, 16)

    imp = dict(allow_small_or_imprecise_dtypes=True)
    blocks = ([[16, 2], [128, 4], [32, 4]], 1), ([[16, 2], [0, 4], [32, 4]], 1), ([[0, 2], [1, 16]], 0), ([[1, 2], [2, 8], [0, 2]], 0)
    BL = [op("g", [], G.iota, T.tb[:, 32 * b:32 * b + 32], pat, 0, cm, **imp) for b, (pat, cm) in enumerate(blocks)]
    ON = op("v", [], V.memset, T.ones[:, :], 1.0)
    SEED = op("v", [ON], V.tensor_tensor_scan, lut(0, 128), T.ones[:, :], T.ones[:, :], -1.0, A.mult, A.add)
    S2 = op("v", [SEED], V.tensor_scalar, lut(128, 256), lut(0, 128), 128.0, None, A.add)
    ZS = op("v", [], V.memset, T.step[:, 128:384], 0.0)
    PAD = op("g", [], G.iota, T.tabi[:, 24:40], [[0, 16]], 0, 0)
    CR0 = op("g", [], G.iota, T.cr0[:, :], [[16, 4], [0, 2]], 0, 0, **imp)
    ID = op("g", [ZS], G.affine_select, T.step[:, 0:128], T.step[:, 128:256], [[-1, 128]], A.not_equal, MARK, 0, 1)
    PEER = [ID]
    for a in range(P):
        PEER.append(op("g", [PEER[-1]], G.iota, T.peer[quarter(a), :], [[0, 1]], 2 * TB * peers[a] + TB - 1 - int(MARK * 2 ** 18), 0, **imp))
    TR = op("g", [PEER], G.iota, T.trash[:, :], [[1, 12]], CAPP + 1, 12, **imp)
    CW0 = op("g", [], G.iota, T.cw[:, 0:CAPP], [[1, CAPP]], NV, 2, **imp)
    SV = op("g", [], G.iota, T.sval[:, :], [[1, P * CAPP]], TB * r + TB, 0, **imp)

    def grow(q, deps, a, n):
        if q == "v":
            return op(q, deps, V.tensor_scalar, lut(a, a + n), lut(0, n), float(a), None, A.add)
        return op(q, deps, S.activation, lut(a, a + n), lut(0, n), AF.Identity, bias=float(a))

    lk = [grow("s", [SEED], a, 128) for a in (1024, 1152)] + [grow("s", [S2], 256 * k, 256) for k in range(5, 10)]
    lk += [grow("v", [S2], 256 * k, 256) for k in range(1, 3)]
    CT = op("v", [BL], V.transpose, T.ct[:, :], T.tb[:, 0:160])
    lk.append(grow("v", [], 768, 256))
    WR = op("v", [CT], V.tensor_scalar, T.wrap[:, :], T.ct[:, 32:33], 128.0, -8.0, A.is_ge, A.mult)
    MK = op("v", [], V.tensor_scalar, T.mask[:, :], lut(0, 32), T.ct[:, 128:129], None, A.is_gt)
    CO = op("v", [WR], V.tensor_scalar, T.coff[:, 0:1], T.ct[:, 0:1], 1.0 / 16, T.wrap[:, 0:1], A.mult, A.add)
    CR = op("v", [CR0], V.tensor_scalar, T.cr[:, :], T.cr0[:, :], T.ct[:, 64:65], None, A.add)

    tab = T.tabi[:, 0:40]
    OK = op("v", [DW], V.tensor_copy, T.offk[:, :], T.tabi[:, 0:24])
    EY = op("v", [CO, PAD], V.tensor_scalar, T.ney[:, :], tab.indirect(T.coff[:, 0:1]), -2.0, None, A.mult)
    win = lut(0, NV)
    DA = op("s", [OK, EY, lk], S.activation, T.da[:, :], win.indirect(T.offk[:, 0:24]), AF.Abs, bias=T.ney[:, 0:1], scale=2.0)
    DC = op("s", [], S.activation, T.sc[:, 384:512], win.indirect(T.offk[:, 16:24]), AF.Abs, bias=T.ney[:, 8:9], scale=2.0)
    DB = op("v", [OK, EY, lk], V.tensor_scalar, T.sc[:, 768:1024], win.indirect(T.offk[:, 8:24]), -2.0, T.ney[:, 4:5], A.mult, A.not_equal)
    HO = op("v", [], V.tensor_copy, T.hoff[:, :], tab.indirect(T.coff[:, 0:1]))
    SB = op("v", [DB, ID], V.tensor_tensor_scan, T.sc[:, 512:768], T.sc[:, 768:1024], T.step[:, 0:256], 0.0, A.min, A.add)
    SA = op("v", [DA], V.tensor_tensor_scan, T.sc[:, 0:384], T.da[:, :], T.step[:, :], 0.0, A.min, A.add)
    TH = op("v", [PEER], V.tensor_scalar, T.th[:, :], T.ney[:, 0:12], T.peer[:, 0:1], -2.0 ** -18, A.add, A.mult)
    SC = op("v", [DC], V.tensor_tensor_scan, T.sc[:, 1024:1152], T.sc[:, 384:512], T.step[:, 0:128], 0.0, A.min, A.add)
    X1 = [op("v", [SA, SB, SC], V.tensor_copy, T.sc[0:64, 575:1440:384], T.sc[64:128, 383:1152:384]),
          op("s", [SA, SB, SC], S.activation, T.sc[64:128, 575:1440:384], T.sc[0:64, 383:1152:384], AF.Copy)]
    X2 = []
    for d in range(P):
        o_, i_ = T.sc[quarter(d), 479:1440:192], T.sc[quarter((d + 1) % P), 383:1344:192]
        X2.append(op("v", [X1], V.tensor_copy, o_, i_) if d % 2 else op("s", [X1], S.activation, o_, i_, AF.Copy))
    IN = op("v", [X2, TH], V.tensor_tensor, T.ind[:, :], T.sc[:, 383:1440:96], T.th[:, :], A.is_equal)
    BG = op("s", [IN], S.activation, T.big[:, :], T.ind[:, :], AF.Identity, bias=4096.0, scale=-4096.0)
    EV = op("s", [HO], S.activation, T.ev[:, :], win.indirect(T.hoff[:, 0:12]), AF.Copy)
    CC = op("v", [IN], V.tensor_tensor_scan, T.cc[:, :], T.ind[:, :], T.step[:, 128:140], 0.0, A.add, A.add)
    RP = op("v", [CC, MK], V.tensor_scalar, T.rp[:, :], T.mask[:, :], T.cc[:, 11:12], None, A.mult)
    P1 = op("v", [BG, TR], V.tensor_tensor, T.p1[:, :], T.big[:, :], T.trash[:, :], A.min)
    RT = op("v", [RP], V.transpose, T.rt[:, :], T.rp[:, :])
    WW = op("v", [P1], V.tensor_tensor, T.ww[:, :], T.cc[:, :], T.p1[:, :], A.add)
    BS = op("v", [RT], V.tensor_reduce, T.base[:, :], T.rt[:, :], X, A.add)
    ZO = op("v", [WW, BS], V.tensor_scalar, T.zo[:, :], T.ww[:, :], T.base[:, 0:1], -1.0, A.add, A.add)
    CW = op("v", [ZO, EV, CW0], V.tensor_copy, T.cw[:, :].indirect(T.zo[:, 0:12]), T.ev[:, :])
    DD = op("v", [CW, CR], V.tensor_copy, T.dd[:, :], T.cw[:, 0:CAPP].indirect(T.cr[:, 0:8]))
    DT = op("v", [DD], V.transpose, T.dtr[:, :], T.dd[:, :])
    LQ = op("v", [DT], V.tensor_tensor, T.lq[:, :], T.dtr[:, 0:128:32], T.dtr[:, 16:128:32], A.min)

    def local(a, d):
        return op("v", [LQ], V.tensor_scalar, T.ls[quarter(d), 4 * a:4 * a + 4], T.lq[quarter(a), :], float(-TB * peers[a]),
                  float(TB - 1), A.add, A.min)

    LS = [local(P - 1, d) for d in range(P)]
    L1 = [local(a, 0) for a in range(P - 1)]
    for k, step in enumerate(STEPS):
        need("g", [LS])
        send([(back[b], T.ls[:, 4 * back[b]:4 * back[b] + 4], T.lin[:, 4 * b:4 * b + 4], T.sem["larr%d" % k]) for b in step], T.sem.lloc)
        if k == 0:
            LS = [op("v", [L1], V.tensor_copy, T.ls[quarter(d), 0:12], T.ls[0:32, 0:12]) for d in range(1, P)]

    XT = [op("s", [DX], S.activation, T.xt[:, TB * t:TB * t + TB], T.xs[:, t:4 * TB:4], AF.Copy) for t in range(4)]
    G0 = [op("s", [LQ], S.activation, T.glf[0:32, 4 * a:4 * a + 4], T.lq[quarter(a), :], AF.Copy) for a in range(P)]
    G1 = [op("s", [G0], S.activation, T.glf[quarter(d), :], T.glf[0:32, :], AF.Copy) for d in range(1, P)]
    C2 = op("v", [], V.tensor_scalar, T.c2[:, :], lut(0, 32, 16), T.ct[:, 96:97], 23.0, A.add, A.min)
    QO = op("v", [DX], V.quantize_mx, T.qo[:, :], T.so[:, :], T.xs[:, :])
    GL = op("v", [G1], V.tensor_copy, T.gl[:, :], T.glf[:, :])
    FD = op("v", [C2], V.tensor_copy, T.fd[:, :], tab.indirect(T.c2[:, 0:2]))
    GS = op("v", [GL, SV, EV], V.tensor_copy, lut(0, NV + P * CAPP).indirect(T.gl[:, 0:16]), T.sval[:, :])
    QW = op("v", [DWT], V.quantize_mx, T.qw[:, :], T.sw[:, :], T.ws[:, :])

    def product(o, out, codes, plane, deps):
        return op("t", deps, M.matmul_mx, out, T.qw[:, 128 * o:128 * o + 128], T.sw[:, 128 * o:128 * o + 128], codes, plane, True, True)

    MO = [product(o, T.pso[:, 512 * o:512 * o + 512], T.qo[:, :], T.so[:, :], [QO, QW]) for o in range(O)]

    for k, step in enumerate(STEPS):
        lo, hi = step[0], step[-1] + 1
        HX, LA, e = [], ("larr%d" % k, ne), 4 * TB + 256 * hi
        for t in range(4):
            o_, i_ = T.xt[:, 4 * TB + 256 * lo + t:e:4], T.xt[:, TB * t:TB * t + TB].indirect(T.lin[:, 4 * lo:4 * hi])
            HX.append(op("v", [LA, XT[t]], V.tensor_copy, o_, i_) if t < 2 else op("s", [LA, XT[t]], S.activation, o_, i_, AF.Copy))
        need("g", [op("v", [HX], V.quantize_mx, T.qx[:, 128 * k:128 * k + 128], T.sx[:, 128 * k:128 * k + 128], T.xt[:, e - 512:e])])
        col = {a: slice(128 * k + 128 - 64 * (hi - a), 128 * k + 192 - 64 * (hi - a)) for a in step}
        sem = T.sem["carr%d" % (k == len(STEPS) - 1)]
        send([(a, T.qx[:, col[a]].bitcast(dt.uint8), T.qr[:, 64 * back[a]:64 * back[a] + 64].bitcast(dt.uint8), sem) for a in step], T.sem.cloc)
        send([(a, T.sx[:, col[a]], T.sr[:, 64 * back[a]:64 * back[a] + 64], sem) for a in step], T.sem.cloc)

    SG = op("s", [GS, FD], S.activation, T.sg[:, :], win.indirect(T.fd[:, 0:24]), AF.Copy)
    PO = [None, op("s", [MO[1]], S.activation, T.py1[:, 0:TB], T.pso[:, 512:1024], AF.Copy)]
    PO[0] = op("v", [MO[0]], V.tensor_copy, T.py0[:, 0:TB], T.pso[:, 0:512])
    SGT = op("v", [SG], V.transpose, T.sgt[:, :], T.sg[:, :])
    YO = op("v", [SGT], V.tensor_scalar, T.yoff[:, :], T.sgt[:, 0:384:16], float(-TB * r), None, A.add)

    PR = [[], []]
    for h, (c, n, new, calls) in enumerate(((64, 192, 192, 2 * len(STEPS) - 2), (0, 128, 64, 2))):
        for o in (1, 0):
            b = 512 * (2 * h + o)
            m = product(o, T.psr[:, b:b + n], T.qr[:, c:c + n], T.sr[:, c:c + n], [("carr%d" % h, calls * ne), QW])
            if o == 0:
                PR[0].append(op("v", [m], V.tensor_copy, T.py0[:, TB + c:TB + c + new], T.psr[:, b:b + new]))
            else:
                PR[1].append(op("s", [m], S.activation, T.py1[:, TB + c:TB + c + new], T.psr[:, b:b + new], AF.Copy))
    nd = 0
    for h, (a, b) in enumerate(((0, 14), (14, 24))):
        c, e = 16 * a, 16 * b
        Y1 = op("s", [PR[1], PO[1], YO], S.activation, T.yo[:, NT + c:NT + e], T.py1[:, :].indirect(T.yoff[:, a:b]), AF.Copy)
        Y0 = op("v", [PR[0], PO[0], YO], V.tensor_copy, T.yo[:, c:e], T.py0[:, :].indirect(T.yoff[:, a:b]))
        for o, tok in ((1, Y1), (0, Y0)):
            q = "s" if h and o else "y"
            need(q, [tok])
            eng[q].dma_start(T.y[:, NT * o + c:NT * o + e], T.yo[:, NT * o + c:NT * o + e]).then_inc(T.sem.dy, 16)
            nd += 16
    need("y", [("dy", nd)])
    need("g", [("lloc", len(STEPS) * ne), ("cloc", 2 * len(STEPS) * ne)] + [("c" + q, cnt[q]) for q in cnt])
